import numpy as np, ml_dtypes
CORES = [1,5,17,21,33,37,49,53]
N = 8
BF = ml_dtypes.bfloat16
M, P, T, H, C, HM = 2304, 256, 4, 3, 48, 2048
E = M + T * P
def crowd(rng, cen, s, n):
    pick = (rng.random((N, 8, 1, n)) * s).astype(np.int64)
    return np.clip(np.take_along_axis(cen, pick, 3) + rng.integers(-1, 2, (N, 8, 16, n)), 0, 15)
def rows(rng):
    v = np.arange(M); i = np.arange(16)[:, None]
    a = np.where(i < rng.integers(2, 17, (N, 8, 1, M)), rng.integers(0, M, (N, 8, 16, M)), E)
    a[:, :, 1] = np.where(v < M - P, v + P, E)
    own = v - P * (1 + (rng.random((N, 8, M)) * (v // P)).astype(np.int64)); low = (rng.random((N, 8, M)) * v).astype(np.int64)
    k = np.where(rng.random((N, 8, M)) < 0.6, own, low)
    a[:, :, 0] = np.where((v < P) | (rng.random((N, 8, M)) < 0.04), E, k)
    return a
def base(rng):
    s = rng.choice(np.array([4, 8, 12, 16, 32]), (N, 8, 1, 1)); cen = np.repeat(rng.integers(0, 16, (1, 8, 16, 32)), N, 0)
    return crowd(rng, cen, s, M), rows(rng), crowd(rng, cen, s, T * P), rng.integers(0, 256, (N, 8, 16, 1)), rng.integers(10, 30, (N, 8, 16, 1))
def pack(f, a, x, w, t):
    return {"fr": np.ascontiguousarray(f.reshape(N, 128, M)).astype(np.float32).astype(BF), "ptr": np.ascontiguousarray(a.reshape(N, 128, M)).astype(np.int32),
            "nw": np.ascontiguousarray(x.reshape(N, 128, T * P)).astype(np.float32).astype(BF),
            "hw": np.ascontiguousarray(w.reshape(N, 128, 1)).astype(np.int32), "th": np.ascontiguousarray(t.reshape(N, 128, 1)).astype(np.int32)}
def setup_inputs(rng):
    return pack(*base(rng))
def setup_inputs_room(rng):
    f, a, x, w, t = base(rng); f = np.minimum(f, 10)
    for q in range(N):
        for g in range(8):
            n = int(rng.choice(np.array([0, 1, C - 1, C, C + 1, P])))
            if q == 0: n = (C, C + 1, P, C - 1, 1, 0, C, C + 1)[g]
            o = rng.permutation(P); esc, rest = o[:n], o[n:]
            k = rng.integers(0, M - P, P - n); a[q, g, 0, M - P + rest] = k; x[q, g][:, rest] = f[q, g][:, k + P]
            a[q, g, 0, M - P + esc] = E
            far = esc[:n // 2]; k = P * rng.integers(1, M // P - 1, len(far)) + far
            a[q, g, 0, M - P + far] = k; a[q, g, 0, k] = k - P; a[q, g, 0, k - P] = E
            x[q, g][:, far] = 15 - rng.integers(0, 2, (16, len(far)))
    return pack(f, a, x, w, t)
def jog(rng, n):
    return (np.arange(16)[:, None] == rng.integers(0, 16, (N, 8, 1, n))) * rng.choice(np.array([-4, 4]), (N, 8, 1, n))
def setup_inputs_ties(rng):
    f, a, x, w, t = base(rng); cen = np.repeat(rng.integers(4, 12, (1, 8, 16, 1)), N, 0)
    f = cen + jog(rng, M); x = cen + jog(rng, T * P) * ((np.arange(T * P) // P) & 1)
    t = rng.integers(3, 6, (N, 8, 16, 1)); t[:, 1::2] = 3
    return pack(f, a, x, w, t)
def setup_inputs_loops(rng):
    f, a, x, w, t = base(rng); v = np.arange(M)
    a[:, :, 2:] = np.where(rng.random((N, 8, 14, M)) < 0.5, rng.integers(0, M, (N, 8, 14, M)), E)
    mate = np.where((((v // P) & 1) == 0) & (v + P < M), v + P, v - P)
    a[:, ::2, 0] = np.where(rng.random((N, 4, M)) < 0.4, v, np.where(rng.random((N, 4, M)) < 0.6, mate, a[:, ::2, 0]))
    a[:, 1, 0] = rng.choice(np.array([0, M - 1, M // 2, E]), (N, M))
    a[:, 3, 2:] = rng.integers(0, M, (N, 14, M)); a[:, 5, 2:] = E; a[:, 7, 2:] = rng.integers(0, M, (N, 1, M))
    return pack(f, a, x, w, t)
def setup_inputs_calm(rng):
    f, a, x, w, t = base(rng); q = [int(c) for c in rng.permutation(8)]
    t[:, q[0]] = 240; a[:, q[0], 0] = np.where(a[:, q[0], 0] == E, rng.integers(0, M, (N, M)), a[:, q[0], 0])
    a[:, q[1], 0] = E
    t[:, q[2]] = 0; f[:, q[2]] = 15 * rng.integers(0, 2, (N, 1, M)); x[:, q[2]] = 15 * rng.integers(0, 2, (N, 1, T * P))
    t[1::2, q[2], 2::2] = 239; t[1::2, q[2], 3::2] = 240
    w[:, q[3]] = 0; w[:, q[4]] = 255
    t[:, q[5]] = 240; t[:, q[5], 1] = 0
    f[:, q[6]] = rng.integers(0, 2, (N, 16, M)); x[:, q[6]] = np.where(((np.arange(T * P) // P) & 1) == 1, 0, 14) + rng.integers(0, 2, (N, 16, T * P))
    a[:, q[6], 0] = np.where(a[:, q[6], 0] < M - P, a[:, q[6], 0], rng.integers(0, M - P, (N, M)))
    w[:, q[6]] = rng.integers(225, 256, (N, 16, 1)); t[:, q[6]] = rng.integers(128, 208, (N, 16, 1))
    f[:, q[7]] = np.abs(15 * rng.integers(0, 2, (N, 1, M)) - rng.integers(0, 2, (N, 16, M)))
    x[:, q[7]] = np.abs(15 * rng.integers(0, 2, (N, 1, T * P)) - rng.integers(0, 2, (N, 16, T * P)))
    a[:, q[7], 0] = np.where(a[:, q[7], 0] == E, rng.integers(0, M, (N, M)), a[:, q[7], 0])
    w[:, q[7]] = rng.integers(128, 256, (N, 16, 1)); t[:, q[7]] = rng.integers(0, 241, (N, 16, 1))
    return pack(f, a, x, w, t)
def setup_inputs_spread(rng):
    f, a, x, w, t = base(rng); e = np.array([0.25, 0.5, 1.0, 1.0, 2.0, 4.0])
    f = np.minimum((16 * rng.random((N, 8, 16, M)) ** rng.choice(e, (N, 8, 1, M))).astype(np.int64), 15)
    x = np.minimum((16 * rng.random((N, 8, 16, T * P)) ** rng.choice(e, (N, 8, 1, T * P))).astype(np.int64), 15)
    a = np.where(rng.random((N, 8, 16, M)) < rng.random((N, 8, 1, M)), rng.integers(0, M, (N, 8, 16, M)), E)
    a[:, :, 0] = np.where(rng.random((N, 8, M)) < 0.1, E, rng.integers(0, M, (N, 8, M)))
    a[:, :, 1, :M - P] = rng.integers(0, M, (N, 8, M - P))
    t = rng.choice(np.array([0, 20, 40, 50, 60, 60, 70, 240]), (N, 8, 16, 1)); t = np.where(rng.random((N, 8, 1, 1)) < 0.5, np.minimum(t, 60), t)
    return pack(f, a, x, w, t)
def check_inputs(d):
    bad = []
    for k in ("fr", "nw"):
        z = d[k].astype(np.float32)
        if not np.all((z >= 0) & (z <= 15) & (z == np.floor(z))): bad.append("whole numbers from 0 to 15 in " + k)
    for k, hi in (("hw", 255), ("th", 240)):
        if np.min(d[k]) < 0 or np.max(d[k]) > hi: bad.append("range of " + k)
    a = d["ptr"]; full = (a >= 0) & (a < M)
    if not np.all(full | (a == E)): bad.append("range of ptr")
    if not np.all(full[:, 1::16, :M - P]): bad.append("row 1 of an old state before the last P is empty")
    return bad
def gaps(F, c, x):
    out = np.empty(c.shape, np.int64)
    for a in range(N):
        for g in range(8): out[a, g] = np.add.reduce(np.abs(F[a, g][:, c[a, g]] - x[a, g][:, None, :]), axis=0)
    return out
def reference(fr, ptr, nw, hw, th):
    F = np.full((N, 8, 16, E + 1), 99, np.int32); F[..., :M] = fr.astype(np.float32).astype(np.int32).reshape(N, 8, 16, M)
    A = np.full((N, 8, 16, E + 1), E, np.int64); A[..., :M] = ptr.reshape(N, 8, 16, M)
    X = nw.astype(np.float32).astype(np.int32).reshape(N, 8, 16, T, P)
    w = hw.astype(np.int64).reshape(N, 8, 16, 1); lim = th.astype(np.int64).reshape(N, 8, 16, 1); piece = np.arange(P)
    for t in range(T):
        n0 = M + P * t; n = n0 + piece; x = X[:, :, :, t]
        F[..., n0:n0 + P] = x; A[:, :, 1, n0 - P:n0] = n
        k = np.array(A[:, :, 0, n0 - P:n0]); link = np.full((N, 8, P), E, np.int64); going = np.ones((N, 8, P), bool)
        for h in range(H):
            c = np.take_along_axis(A, k[:, :, None, :], 3)
            ok = (gaps(F, c, x) <= lim) & (c < E); ok[:, :, 0] = False
            hit = np.any(ok, axis=2); to = np.take_along_axis(c, np.argmax(ok, axis=2)[:, :, None, :], 2)[:, :, 0]
            link = np.where(going & hit, to, link); going = going & ~hit
            free = c == E; free[:, :, 0] = False
            wr = going & (k < E) & ((k & (P - 1)) == piece) & np.any(free, axis=2)
            a, g, p = np.nonzero(wr); A[a, g, np.argmax(free, axis=2)[wr], k[wr]] = n[p]
            k = np.where(going, c[:, :, 0], k)
        A[:, :, 0, n0:n0 + P] = np.where(going, k, link)
        if t < T - 1:
            for a in range(N):
                b = (a + 1 + t % (N - 1)) % N
                for g in range(8):
                    ps = np.nonzero(going[a, g])[0][:C]; z = x[a, g][:, ps].astype(np.int64)
                    q = np.add.reduce(w[b, g] * z, axis=0) & (HM - 1)
                    c = A[b, g][1:, q]
                    best = np.argmin(np.add.reduce(np.abs(F[b, g][:, c] - z[:, None, :]), axis=0), axis=0)
                    f = F[b, g][:, c[best, np.arange(len(ps))]]
                    X[a, g][:, t + 1, ps] = (X[a, g][:, t + 1, ps] + f) >> 1
    return {"yp": np.ascontiguousarray(A[..., :E]).reshape(N, 128, E).astype(np.float32), "yx": X.reshape(N, 128, T * P).astype(np.float32).astype(BF)}

@@ -1,0 +1,609 @@
+from concourse.mybir import AluOpType as OP, AxisListType as AX, ActivationFunctionType as AF
+
+N, M, P, NT, E = 8, 2304, 256, 4, 3328
+DUM = 3336
+AW = DUM + P
+XW = 320
+SW = 304
+BIG, FRZ = float(1 << 22), float(1 << 21)
+CH = 64
+MODES = ["BBRRRRRRLLLL"]
+CFG = {"split": 2, "prem": 2000.0}
+ROUNDS = 3
+
+f32, b16, i32, u16 = "float32", "bfloat16", "int32", "uint16"
+SB = {
+    "PT": (M, i32), "A": (AW, f32), "F": (3336, b16), "XS": (NT * XW, b16), "xrep": (NT * 4096, b16),
+    "thi": (4, i32), "hwi": (4, i32), "pi": (4, i32), "ri": (4, i32), "K": (40, f32),
+    "J": (256, f32), "JG": (128, f32), "JR": (128, f32), "NA": (1024, f32), "NK": (1088, f32), "EN": (1024, f32),
+    "CW": (256, f32), "CT": (256, f32), "CK": (768, f32), "TA": (768, b16), "TB": (768, b16), "PW": (48, f32), "DP": (48, f32),
+    "SO": (48, u16), "ONE": (SW, b16),
+    "Sel": (144, b16), "Sel2": (144, b16), "Seln": (144, b16), "I": (128, b16), "In": (128, b16), "BO": (128, b16),
+    "BOf": (128, f32), "S0f": (128, f32), "S0b": (128, b16), "S0n": (128, b16), "S0h": (128, b16), "BOw": (128, b16),
+    "BOk": (128, b16), "BO4": (128, b16), "HS": (128, b16), "HS2": (128, b16), "S0k": (128, b16), "ZT": (128, b16),
+    "ZTh": (128, b16), "TriF": (128, b16),
+    "Ir": (128, b16), "m1": (128, b16), "m2": (128, b16), "m3": (128, b16), "m4": (128, b16), "m5": (128, b16),
+    "scn": (768, f32), "kw": (48, u16), "ki": (48, i32), "lo": (48, i32), "ow": (48, u16), "s1": (48, f32), "s2": (48, f32),
+    "s3": (48, f32), "sc": (48, u16), "cb": (832, f32), "cu": (768, u16), "fs": (1024, b16), "cval": (768, f32),
+    "d": (4 * 1024, b16), "ad": (4 * 1024, b16), "G": (4096, b16), "Gs": (2048, b16), "ab": (1024, b16), "sg": (3 * SW, b16),
+    "xc": (P, b16), "d0": (768, b16), "a0": (768, b16), "r0": (768, b16), "okn": (768, b16), "e": (768, b16), "gs": (768, b16),
+    "Kw": (2 * XW, f32), "y": (768, f32), "dlt": (768, f32),
+    "esc": (SW, b16), "cnt": (SW, b16), "jk": (3 * SW, b16), "acc": (4, f32), "pl": (4, u16),
+    "msg": (3 * 48, b16), "req": (3 * 48, b16), "out": (3 * 48, b16), "rep": (3 * 48, b16),
+    "qs": (48, f32), "qi": (4, i32), "qj": (4, i32), "qw": (4, u16), "cq": (48, u16), "xq": (768, b16), "dq": (768, b16),
+    "aq": (768, b16), "ks": (768, f32), "bi": (4, i32), "bj": (4, i32), "bw": (4, u16),
+    "xo": (48, f32), "xs": (48, b16), "xn": (144, b16), "cua": (144, u16), "Ga": (2304, b16), "sga": (144, b16),
+}
+PS = {"PB": 2048, "PD": 1024, "PM": 1024}
+SCRATCH = {k: ("sbuf", [128, w], t) for k, (w, t) in SB.items()}
+SCRATCH.update({k: ("psum", [128, w], f32) for k, w in PS.items()})
+SEMAPHORES = ["V", "S", "T", "G", "lo"] + ["q%d" % t for t in range(3)] + ["a%d" % t for t in range(3)] + ["d%d" % i for i in range(40)]
+
+(RF, GB, PF, G15, M0, N0M, M1E, OFW, OF7, TH, BSG, R0S, R0B, FB0, FB1, FB2, FB3, BZ1, BZ2, BZ3, BW, LB, SL0, SL1, SL2,
+ NKB, HW, HSC, RP1, T1, T2, T3, T4, T5, T6, T7) = range(36)
+
+
+def v(n, lo=0, hi=None, st=1, p=None):
+    if hi is None:
+        hi = (SB[n][0] if n in SB else PS[n])
+    return {"n": n, "lo": lo, "hi": hi, "st": st, "p": p, "w": len(range(lo, hi, st))}
+
+
+def kc(c):
+    return v("K", c, c + 1)
+
+
+def ind(win, off):
+    return {"win": win, "off": off, "w": 16 * off["w"], "n": win["n"]}
+
+
+def size(a):
+    return 4 if a["n"] in PS or SB[a["n"]][1] in (f32, i32) else 2
+
+
+REF = {"cyc": 1.04, "g": 1.56, "s": 3.8, "pe": 0.52, "lat": 110.0, "rem": 4000.0, "dma": 2200.0, "bw": 100.0, "tt": 2.0}
+OTHERS = [{}, {"g": 1.15, "s": 2.2}, {"g": 2.0, "s": 5.5}, {"pe": 0.7}, {"rem": 7000.0, "lat": 200.0}]
+
+
+def cost(o, c):
+    k, a = o["k"], o["a"]
+    if k == "dma":
+        return 60.0
+    if k in ("send", "arrive"):
+        return 500.0 if k == "send" else 0.0
+    if k == "mm":
+        return max(64, a[2]["w"]) * c["pe"] * (4 if size(a[2]) == 4 else 1) + 10
+    w = a[0]["w"]
+    if k == "iota":
+        return 130 + 2 * w * c["cyc"]
+    if k == "sel":
+        return 170 + 2 * w * c["cyc"]
+    if "win" in a[0]:
+        return 50 + c["s"] * w * c["cyc"]
+    if k != "set" and "win" in a[1]:
+        return 60 + c["g"] * w * c["cyc"]
+    if k == "act":
+        return 65 + max(64, w) * c["cyc"]
+    if k == "red":
+        return 40 + max(64, a[1]["w"]) * c["cyc"]
+    aps = [x for x in a if isinstance(x, dict) and x["w"] == w]
+    f = 0.5 if all(size(x) == 2 for x in aps) else 1.0
+    if k == "tt":
+        f = 1.0 if any(x["n"] in PS for x in aps[1:]) else c["tt"]
+    return 40 + max(64, w * f) * c["cyc"]
+
+
+def program(modes):
+    L = []
+
+    def op(eng, k, *a):
+        L.append({"e": eng, "k": k, "a": a})
+
+    def ts(out, x, s1, o1, s2=None, o2=None): op("V", "ts", out, x, s1, o1, s2, o2)
+    def tt(out, x, y, o): op("V", "tt", out, x, y, o)
+    def cp(out, x): op("V", "cp", out, x)
+    def mset(out, c): op("V", "set", out, c)
+    def scan(out, d0, d1, o0, o1): op("V", "scan", out, d0, d1, o0, o1)
+    def act(out, x, f, bias=0.0, scale=1.0, acc=None): op("S", "act", out, x, f, bias, scale, acc)
+    def mm(out, l, r, st, sp): op("T", "mm", out, l, r, st, sp)
+    def grp(out, terms):
+        for i, (l, r) in enumerate(terms):
+            mm(out, l, r, i == 0, i == len(terms) - 1)
+    def iota(out, pat, base, cm): op("G", "iota", out, pat, base, cm)
+    def dma(q, out, x, nbytes, after=None): op(q, "dma", out, x, nbytes, after)
+    ID = AF.Identity
+    nh = 2 if modes[8:] == "LLLL" else 3
+
+    dma("Q", v("PT", 2048, M), ("ptr", 2048, M), 128 * 1024)
+    dma("S", v("F", M, M + P), ("nw", 0, P), 128 * 512)
+    dma("Q", v("PT", 0, 1024), ("ptr", 0, 1024), 128 * 4096)
+    dma("S", v("PT", 1024, 2048), ("ptr", 1024, 2048), 128 * 4096)
+    dma("Q", v("F", 0, M), ("fr", 0, M), 128 * 4608)
+    dma("S", v("F", M + P, E), ("nw", P, 1024), 128 * 1536)
+    iota(v("pi", 0, 1), [[0, 1]], 0, 1)
+    iota(v("JG"), [[16, 8], [0, 16]], 0, 0)
+    iota(v("JR"), [[0, 8], [1, 16]], 0, 0)
+    iota(v("J"), [[1, 256]], 0, 0)
+    iota(v("CT"), [[0, 16], [1, 16]], 0, 0)
+    iota(v("PW"), [[0, 3], [16, 16]], 0, 0)
+    iota(v("NA"), [[1, 1024]], M, 0)
+    ts(v("ri", 0, 1), v("pi", 0, 1), 15, OP.bitwise_and)
+    cp(kc(RF), v("ri", 0, 1))
+    cp(kc(PF), v("pi", 0, 1))
+    tt(kc(GB), kc(PF), kc(RF), OP.subtract)
+    ts(kc(M0), kc(RF), 0.0, OP.is_equal)
+    ts(kc(M1E), kc(RF), 1.0, OP.is_equal, float(E), OP.mult)
+    ts(kc(OFW), kc(RF), 15.0, OP.is_lt, FRZ, OP.mult)
+    act(kc(RP1), kc(RF), ID, bias=1.0)
+    act(kc(G15), kc(GB), ID, bias=15.0)
+    act(kc(N0M), kc(M0), ID, bias=1.0, scale=-1.0)
+    act(kc(OF7), kc(OFW), ID, bias=768.0)
+    ts(v("BO"), v("JG"), kc(GB), OP.is_equal)
+    act(v("S0f"), v("BO"), ID, scale=kc(M0))
+    ts(v("CW"), v("CT"), kc(RF), OP.is_equal, BIG, OP.mult)
+    ts(v("CT"), v("CT"), kc(RP1), OP.is_equal, -FRZ, OP.mult)
+    tt(v("CW"), v("CW"), v("CT"), OP.add)
+    mset(v("A", M, AW), float(E))
+    mset(v("F", E, 3336), 99.0)
+    ts(v("A", 2048, M), v("PT", 2048, M), kc(M1E), OP.max)
+    for lo in (0, 512, 1024, 1536):
+        cp(v("A", lo, lo + 512), v("PT", lo, lo + 512))
+    dma("Q", v("thi", 0, 1), ("th", 0, 1), 20000, v("A", 0, 8))
+    dma("Q", v("hwi", 0, 1), ("hw", 0, 1), 20000, v("A", 0, 8))
+    for t in range(NT):
+        dma("Q", v("XS", XW * t, XW * t + P), ("nw", P * t, P * t + P), 128 * 512, v("A", 0, 8))
+    ts(v("Sel"), v("J", 0, 144), kc(G15), OP.is_equal)
+    act(v("Sel2"), v("Sel"), ID, scale=2.0)
+    act(v("Seln"), v("Sel"), ID, scale=-1.0)
+    ts(v("I"), v("J", 0, 128), kc(PF), OP.is_equal)
+    act(v("In"), v("I"), ID, scale=-1.0)
+    for i in range(16):
+        if i % 3 == 2:
+            act(v("xrep", i, 4096, 16), v("F", M, M + P), ID)
+        else:
+            cp(v("xrep", i, 4096, 16), v("F", M, M + P))
+    cp(kc(TH), v("thi", 0, 1))
+    cp(kc(HW), v("hwi", 0, 1))
+    act(kc(BSG), kc(TH), ID, bias=0.5)
+    act(kc(R0S), kc(N0M), ID, scale=16.0)
+    act(kc(T1), kc(TH), ID, scale=kc(R0S))
+    act(kc(R0B), kc(T1), ID, scale=-1.0, bias=kc(M0))
+    for t in range(NT):
+        act(kc(FB0 + t), kc(M0), ID, scale=float(E - (M + P * t - P)), bias=0.5 - E)
+    act(kc(T2), kc(RF), ID, scale=-0.5, bias=1.0)
+    act(kc(BZ1), kc(M0), ID, scale=-200.0, bias=kc(T2))
+    act(kc(BZ2), kc(BZ1), ID, bias=-2048.0)
+    act(kc(T4), kc(M0), ID, scale=-7.5, bias=kc(T2))
+    act(kc(BZ3), kc(T4), ID, bias=-2048.0)
+    act(kc(T5), kc(RF), ID, scale=-2048.0, bias=-4096.0 * 6.5)
+    act(kc(BW), kc(M0), ID, scale=-1.0e6, bias=kc(T5))
+    act(kc(LB), kc(N0M), ID, scale=float(E))
+    for b in range(3):
+        act(kc(SL0 + b), kc(RF), ID, bias=16.0 * b + 0.5)
+    act(kc(NKB), kc(M0), ID, scale=4000.0)
+    act(kc(HSC), kc(M0), ID, scale=30720.0 - 2048.0, bias=2048.0)
+    act(kc(T6), kc(M0), ID, scale=30720.0, bias=2048.0)
+    act(v("NK", 0, 1024), v("NA"), ID, scale=kc(N0M), bias=kc(NKB))
+    mset(v("NK", 1024, 1088), 4000.0)
+    iota(v("EN"), [[-1, 1024]], E - M, 0)
+    iota(v("TA"), [[16, 48], [0, 16]], 0, 0)
+    iota(v("TB"), [[0, 48], [1, 16]], 0, 0)
+    mset(v("TB", 0, 768, 16), 1.75 * (1 << 20))
+    ts(v("PW"), v("PW"), kc(RF), OP.add)
+    act(v("DP"), v("PW"), ID, bias=float(DUM + 768))
+    cp(v("SO"), v("J", 0, 48))
+    mset(v("ONE"), 1.0)
+    mset(v("cb", 768, 832), 0.0)
+    mset(v("esc", P, SW), 1.0)
+    mset(v("Kw", P, XW), -1.0)
+    mset(v("Kw", XW + P, 2 * XW), -1.0)
+    act(v("CK"), v("NA", 0, 768), ID, scale=0.0)
+    cp(v("CK", 0, 768, 16), v("CW", 0, 48))
+    for t in range(NT):
+        mset(v("XS", XW * t + P, XW * t + SW), 0.0)
+        mset(v("XS", XW * t + SW, XW * t + XW), 99.0)
+    for name, sc_ in (("BOf", 1.0), ("S0b", kc(M0)), ("BOw", kc(HW)), ("BOk", 1024.0), ("BO4", 4096.0), ("HS", kc(HSC)),
+                      ("HS2", kc(T6))):
+        act(v(name), v("BO"), ID, scale=sc_)
+    act(v("S0n"), v("S0b"), ID, scale=-1.0)
+    act(v("S0h"), v("S0b"), ID, scale=-0.5)
+    act(v("S0k"), v("S0b"), ID, scale=-2048.0)
+    ts(v("m1"), v("JR"), kc(RF), OP.is_gt, kc(N0M), OP.mult)
+    tt(v("m1"), v("m1"), v("BO"), OP.mult)
+    act(v("m2"), v("I"), ID, scale=kc(N0M))
+    act(v("m3"), v("m2"), ID, scale=-16.0)
+    tt(v("m3"), v("m3"), v("m1"), OP.add)
+    act(v("TriF"), v("m3"), ID, scale=0.5)
+    ts(v("m4"), v("JR"), 0.0, OP.is_equal, kc(N0M), OP.mult)
+    tt(v("m4"), v("m4"), v("BO"), OP.mult)
+    tt(v("m4"), v("m4"), v("m1"), OP.add)
+    tt(v("ZT"), v("m4"), v("m2"), OP.subtract)
+    act(v("ZTh"), v("ZT"), ID, scale=0.5)
+    act(v("m5"), v("JR"), ID, scale=0.5, bias=7.0)
+    tt(v("m5"), v("m5"), v("S0b"), OP.mult)
+    tt(v("Ir"), v("m5"), v("m2"), OP.add)
+
+    def sel(n, i): return v(n, 15 - i, 143 - i)
+    def blk(n, h, w=P): return v(n, w * h, w * h + P)
+    def bank(n, b): return v(n, 512 * b, 512 * b + P)
+    def ow(h): return v("ow", 16 * h, 16 * h + 16)
+    AG, FG = v("A", 0, E + 1), v("F", 0, E + 1)
+    fill = [0]
+
+    def by_pe(gbuf, g0, n, x, dout):
+        rows = list(range(1, 16))
+        while rows:
+            now, rows = rows[:512 // n], rows[512 // n:]
+            hb = 512 * (fill[0] % 2)
+            fill[0] += 1
+            for j, i in enumerate(now):
+                grp(v("PB", hb + n * j, hb + n * j + n), [(v("In"), x), (v("I"), v(gbuf, g0 + i, g0 + 16 * n, 16))])
+            act(v("ab", hb, hb + n * len(now)), v("PB", hb, hb + n * len(now)), AF.Abs)
+            for j, i in enumerate(now):
+                mm(dout, sel("Sel", i), v("ab", hb + n * j, hb + n * j + n), i == 1, i == 15)
+
+    def wrap(h, src):
+        scan(blk("scn", h), v("CW"), src, OP.add, OP.min)
+        ts(v("kw", 16 * h, 16 * h + 16), v("scn", P * h + 15, P * h + P, 16), kc(OFW), OP.add)
+
+    link = bank("PB", 3)
+    grp(link, [(v("S0f"), v("A", 2048, M))])
+    nd = [0, 0]
+    for t in range(NT):
+        n0 = M + P * t
+        X = v("XS", XW * t, XW * t + XW)
+        x = v("XS", XW * t, XW * t + P)
+        prev = v("A", n0 - P, n0)
+        wrap(0, link)
+        if t > 0:
+            act(prev, link, ID, scale=kc(M0), bias=kc(LB))
+        for h in range(3):
+            act(blk("cb", h), ind(AG, v("kw", 16 * h, 16 * h + 16)), ID)
+            cp(blk("cu", h), blk("cb", h))
+            if h < 2:
+                kb = bank("PB", 2)
+                grp(kb, [(v("S0f"), blk("cb", h))])
+                wrap(h + 1, kb)
+        act(blk("fs", 0), prev, AF.Sign, bias=kc(FB0 + t))
+        dma("Q", v("A", n0 - P, n0, 1, (1, 128, 16)), v("NK", P * t, P * t + P, 1, (1, 128, 16)), 30000)
+        act(v("fs", P, 1024), v("cb", 0, 768), AF.Sign, bias=kc(FB0 + t))
+        ts(v("ki"), v("scn", 15, 768, 16), kc(OF7), OP.add)
+        ts(v("lo"), v("ki"), 0x10FF, OP.bitwise_and)
+        ts(v("ow"), v("lo"), 304.0, OP.min)
+        tt(v("s1"), v("lo"), v("PW"), OP.not_equal)
+        tt(v("s2"), v("s1"), v("DP"), OP.mult)
+        tt(v("s3"), v("s2"), v("ki"), OP.max)
+        ts(v("sc"), v("s3"), -768.0, OP.add)
+        for h in range(3):
+            tt(blk("cval", h), ind(v("NK", P * t, P * t + XW), ow(h)), blk("cb", h), OP.min)
+        if t > 0:
+            rq = v("req", 48 * t - 48, 48 * t)
+            op("X", "arrive", rq, "q%d" % (t - 1))
+            qp = v("PM", 0, 48)
+            grp(qp, [(v("BOw"), rq)])
+            scan(v("qs"), v("CW", 0, 48), qp, OP.add, OP.min)
+            ts(v("qi", 0, 3), v("qs", 15, 48, 16), kc(OFW), OP.add)
+            ts(v("qj", 0, 3), v("qi", 0, 3), 2047, OP.bitwise_and)
+            cp(v("qw", 0, 3), v("qj", 0, 3))
+            cp(v("cq"), ind(v("A", 0, 2048), v("qw", 0, 3)))
+            for lo, hi in ((0, 512), (512, 768)):
+                act(v("xq", lo, hi), ind(rq, v("SO", lo // 16, hi // 16)), ID)
+                tt(v("dq", lo, hi), ind(FG, v("cq", lo // 16, hi // 16)), v("xq", lo, hi), OP.subtract)
+                act(v("aq", lo, hi), v("dq", lo, hi), AF.Abs)
+                grp(v("PM", lo, hi), [(v("S0b"), v("TA", lo, hi)), (v("S0b"), v("TB", lo, hi)), (v("BOk"), v("aq", lo, hi))])
+                scan(v("ks", lo, hi), v("CK", lo, hi), v("PM", lo, hi), OP.add, OP.min)
+            ts(v("bi", 0, 3), v("ks", 255, 768, 256), kc(OFW), OP.add)
+            ts(v("bj", 0, 3), v("bi", 0, 3), 1023, OP.bitwise_and)
+            cp(v("bw", 0, 3), v("bj", 0, 3))
+            ro = v("out", 48 * t - 48, 48 * t)
+            tt(ro, ind(v("dq"), v("bw", 0, 3)), rq, OP.add)
+            op("G", "send", v("rep", 48 * t - 48, 48 * t), ro, "a%d" % (t - 1), -(1 + (t - 1) % (N - 1)))
+            pl = v("pl", 0, 3)
+            ts(v("xo"), ind(X, pl), 383.5, OP.add)
+            for h in range(nh):
+                cp(v("cua", 48 * h, 48 * h + 48), ind(v("cb", P * h, P * h + SW), pl))
+                act(v("Ga", 768 * h, 768 * h + 768), ind(FG, v("cua", 48 * h, 48 * h + 48)), ID)
+        if t + 1 < NT:
+            for i in range(16):
+                o = 4096 * (t + 1)
+                op("G", "sel", v("xrep", o + i, o + 4096, 16), v("F", n0 + P, n0 + 2 * P))
+        dh = [v("PD", 0, P), v("PD", 512, 512 + P), v("PD", P, 2 * P)]
+        late = []
+        for h in range(3):
+            for c in range(P // CH):
+                s0, mode = CH * c, modes[h * (P // CH) + c]
+                dout = v("PD", dh[h]["lo"] + s0, dh[h]["lo"] + s0 + CH)
+                if mode in "BL":
+                    buf, o = ("Gs", 1024 * (nd[1] % 2)) if mode == "B" else ("G", 16 * s0)
+                    for u in (0, 32):
+                        act(v(buf, o + 16 * u, o + 16 * u + 512), ind(FG, v("cu", P * h + s0 + u, P * h + s0 + u + 32)), ID)
+                    if mode == "B":
+                        nd[1] += 1
+                        by_pe("Gs", o, CH, v("F", n0 + s0, n0 + s0 + CH), dout)
+                    else:
+                        late.append((s0, dout))
+                    continue
+                o = 1024 * (nd[0] % 4)
+                nd[0] += 1
+                d, ad = v("d", o, o + 16 * CH), v("ad", o, o + 16 * CH)
+                w = CH // CFG["split"]
+                for u in range(0, CH, w):
+                    tt(v("d", o + 16 * u, o + 16 * (u + w)), ind(FG, v("cu", P * h + s0 + u, P * h + s0 + u + w)),
+                       v("xrep", 4096 * t + 16 * (s0 + u), 4096 * t + 16 * (s0 + u + w)), OP.subtract)
+                if mode == "A":
+                    act(ad, d, AF.Abs)
+                    grp(dout, [(sel("Sel", i), v("ad", o + i, o + 16 * CH, 16)) for i in range(1, 16)])
+                else:
+                    ts(ad, d, 0.0, OP.max)
+                    grp(dout, [(sel("Seln", i), v("d", o + i, o + 16 * CH, 16)) for i in range(1, 16)]
+                        + [(sel("Sel2", i), v("ad", o + i, o + 16 * CH, 16)) for i in range(1, 16)])
+            if not late:
+                act(blk("sg", h, SW), dh[h], AF.Sign, bias=kc(BSG), scale=-1.0)
+        if t > 0:
+            rp = v("rep", 48 * t - 48, 48 * t)
+            op("X", "arrive", rp, "a%d" % (t - 1))
+            tt(v("xs"), v("xo"), rp, OP.add)
+            for h in range(nh):
+                ts(v("xn", 48 * h, 48 * h + 48), v("xs"), 0.5, OP.mult, -192.0, OP.add)
+            cp(ind(X, pl), v("xn", 0, 48))
+            da = v("PB", 1536, 1536 + 48 * nh)
+            by_pe("Ga", 0, 48 * nh, v("xn", 0, 48 * nh), da)
+            act(v("sga", 0, 48 * nh), da, AF.Sign, bias=kc(BSG), scale=-1.0)
+            for h in range(2):
+                cp(ind(v("sg", SW * h, SW * h + SW), pl), v("sga", 48 * h, 48 * h + 48))
+        dma("Q", ("yx", P * t, P * t + P), x, 128 * 512)
+        cp(v("xc"), x)
+        for h in range(3):
+            tt(blk("d0", h), ind(X, ow(h)), v("xc"), OP.subtract)
+            act(blk("a0", h), blk("d0", h), AF.Abs)
+            grp(bank("PM", h % 2), [(v("BO"), blk("a0", h))])
+            act(blk("r0", h), bank("PM", h % 2), AF.Relu, bias=kc(R0B), scale=kc(R0S))
+        for s0, dout in late:
+            by_pe("G", 16 * s0, CH, v("XS", XW * t + s0, XW * t + s0 + CH), dout)
+        if late:
+            act(blk("sg", 2, SW), dh[2], AF.Sign, bias=kc(BSG), scale=-1.0)
+        if t > 0 and nh == 3:
+            cp(ind(v("sg", SW * 2, SW * 3), pl), v("sga", 96, 144))
+        if t + 1 < NT:
+            cp(v("F", n0, n0 + P), x)
+        U = [bank("PM", 0), bank("PD", 1), bank("PM", 1)]
+        H = [bank("PM", 1), bank("PM", 0), bank("PD", 1)]
+        Z = [bank("PB", 2), bank("PB", 2), bank("PM", 0)]
+        W = [bank("PB", 3), bank("PB", 3), bank("PB", 2)]
+        es = [[], [0], [1, 2]]
+        for h in range(3):
+            col = [(v("TriF"), blk("fs", h + 1)), (v("S0h"), blk("fs", h))]
+            wr = [(v("S0n"), blk("e", j)) for j in es[h]]
+            grp(U[h], col + [(v("Ir"), blk("r0", h))] + wr)
+            ts(blk("okn", h), U[h], -0.5, OP.is_lt)
+            old = [(v("S0k"), blk("gs", h - 1))] if h else []
+            grp(H[h], old + [(v("HS2" if h else "HS"), blk("sg", h, SW)), (v("BO4"), blk("okn", h))])
+            if h < 2:
+                kwin = v("Kw", XW * h, XW * h + XW)
+                tt(blk("Kw", h, XW), H[h], prev if h == 0 else blk("cb", 0), OP.add)
+                if h == 0:
+                    tt(blk("e", 0), ind(kwin, ow(1)), blk("cb", 0), OP.is_equal)
+                tt(blk("e", 1 + h), ind(kwin, ow(2)), blk("cb", 1), OP.is_equal)
+            elif t + 1 < NT:
+                ts(v("esc", 0, P), H[2], 0.5, OP.is_lt)
+                scan(v("cnt"), v("ONE"), v("esc"), OP.mult, OP.add)
+                for b in range(2):
+                    act(v("jk", SW * b, SW * b + SW), v("cnt"), AF.Sign, bias=kc(SL0 + b), scale=-1.0, acc=v("acc", b, b + 1))
+                ts(v("jk", 2 * SW, 3 * SW), v("cnt"), kc(SL2), OP.is_le, 2.0, OP.mult)
+                op("V", "red", kc(T7), v("jk", 2 * SW, 3 * SW))
+                ts(v("acc", 2, 3), kc(T7), -float(SW), OP.add)
+                ts(v("pl", 0, 3), v("acc", 0, 3), 0.5, OP.mult, SW / 2.0, OP.add)
+                ms = v("msg", 48 * t, 48 * t + 48)
+                cp(ms, ind(X, v("pl", 0, 3)))
+                op("G", "send", v("req", 48 * t, 48 * t + 48), ms, "q%d" % t, 1 + t % (N - 1))
+            act(blk("gs", h), H[h], AF.Sign, bias=0.5, scale=-1.0)
+            grp(Z[h], old + [(v("ZTh"), blk("sg", h, SW)), (v("ZT"), blk("okn", h))])
+            act(Z[h], Z[h], AF.Relu, bias=kc(BZ1 + h), scale=-1.0)
+            tt(blk("y", h), Z[h], blk("cval", h), OP.mult)
+            grp(W[h], col + wr + [(v("S0h"), blk("gs", h))])
+            act(W[h], W[h], AF.Relu, bias=kc(BW), scale=-4096.0)
+            tt(blk("dlt", h), W[h], blk("EN", t), OP.min)
+            tt(ind(v("A"), v("sc", 16 * h, 16 * h + 16)), blk("cb", h), blk("dlt", h), OP.subtract)
+        grp(link, [(v("BOf"), blk("y", h)) for h in range(3)])
+    act(v("A", E - P, E), link, ID, scale=kc(M0), bias=kc(LB))
+    for q, lo, hi in (("Q", 0, 1536), ("S", 1536, 3072), ("Q", 3072, E)):
+        dma(q, ("yp", lo, hi), v("A", lo, hi), 128 * 4 * (hi - lo))
+    return L
+
+
+def touches(o):
+    res = []
+
+    def add(a, w):
+        if not isinstance(a, dict):
+            return
+        if "win" in a:
+            add(a["win"], w)
+            add(a["off"], False)
+        elif a["n"] in PS:
+            res.append((a["n"], a["lo"] // 512 * 512, (a["hi"] + 511) // 512 * 512, True, 1, True))
+        else:
+            res.append((a["n"], a["lo"], a["hi"], w, a["st"], a["p"] is None))
+    a = o["a"]
+    if o["k"] != "send":
+        add(a[0], True)
+    for i, x in enumerate(a[1:]):
+        add(x, o["k"] == "act" and i == 4)
+    return res
+
+
+def clash(x, y):
+    if x[1] >= y[2] or y[1] >= x[2] or not (x[3] or y[3]):
+        return False
+    return not (x[4] == y[4] and x[4] > 1 and (x[1] - y[1]) % x[4] != 0)
+
+
+def depend(L):
+    seen, sent = {}, {}
+    for i, o in enumerate(L):
+        deps = set()
+        tch = touches(o)
+        for x in tch:
+            for y, j in seen.get(x[0], []):
+                if clash(x, y):
+                    deps.add(j)
+        for x in tch:
+            old = seen.get(x[0], [])
+            if x[3] and x[4] == 1 and x[5]:
+                old = [(y, j) for y, j in old if not (x[1] <= y[1] and y[2] <= x[2])]
+            seen[x[0]] = old + [(x, i)]
+        deps.discard(i)
+        if o["k"] == "send":
+            sent[o["a"][2]] = i
+        o["deps"] = sorted(deps)
+        o["peer"] = sent[o["a"][1]] if o["k"] == "arrive" else None
+    return L
+
+
+def schedule(L, c, fixed, rounds=0):
+    n = len(L)
+    dur = [cost(o, c) for o in L]
+    late = [c["dma"] + o["a"][2] / c["bw"] if o["k"] == "dma" else 0.0 for o in L]
+    pre, suc = [], [[] for _ in L]
+    for i, o in enumerate(L):
+        pre.append([(j, 0.0 if o["e"] == "T" and L[j]["e"] == "T" else c["lat"] + late[j]) for j in o["deps"]]
+                   + ([(o["peer"], c["rem"])] if o["peer"] is not None else []))
+        for j, w in pre[i]:
+            suc[j].append((i, w))
+    if fixed is not None:
+        fin, free = [0.0] * n, {}
+        for i in fixed:
+            st = max([free.get(L[i]["e"], 0.0)] + [fin[j] + w for j, w in pre[i]])
+            fin[i] = free[L[i]["e"]] = st + dur[i]
+        return fin, max(fin[i] + late[i] for i in range(n))
+
+    def place(seq, before, head):
+        busy, fin = {}, [0.0] * n
+        for i in seq:
+            st = max([head[i]] + [fin[j] + w for j, w in before[i]])
+            slots = busy.setdefault(L[i]["e"], [])
+            at = len(slots)
+            while at > 0 and slots[at - 1][1] > st:
+                at -= 1
+            while at < len(slots) and slots[at][0] < st + dur[i]:
+                st = max(st, slots[at][1])
+                at += 1
+            slots.insert(at, (st, st + dur[i]))
+            fin[i] = st + dur[i]
+        return fin
+    prio = [dur[i] + late[i] + 0.001 for i in range(n)]
+    for i in range(n - 1, -1, -1):
+        for j, w in pre[i]:
+            prio[j] = max(prio[j], dur[j] + (CFG["prem"] if L[i]["peer"] == j else w) + prio[i] + 0.001)
+    res = []
+    for r in range(rounds + 1):
+        fin = place(sorted(range(n), key=lambda i: (-prio[i], i)), pre, [0.0] * n)
+        res.append(sorted(range(n), key=lambda i: (fin[i] - dur[i], fin[i], i)))
+        prio = place(sorted(range(n), key=lambda i: (-fin[i], dur[i] - fin[i], -i)), suc, late)
+    return res
+
+
+def plan():
+    best = None
+    for modes in MODES:
+        L = depend(program(modes))
+        for r, order in enumerate(schedule(L, REF, None, ROUNDS)):
+            end = sum(schedule(L, dict(REF, **c), order)[1] for c in OTHERS) / len(OTHERS)
+            if best is None or end < best[2]:
+                best = (L, order, end, modes, r)
+    return best
+
+
+PLAN = []
+
+
+def rank_program(g, core, T, topo):
+    rank = T.rank_of(core)
+    if rank is None:
+        return
+    if not PLAN:
+        PLAN.append(plan())
+    L, order = PLAN[0][0], PLAN[0][1]
+    Q = {"V": g.vector, "S": g.scalar, "T": g.tensor, "G": g, "Q": g.sync}
+
+    def ap(a):
+        if isinstance(a, tuple):
+            return T[a[0]][:, a[1]:a[2]] if a[0] not in ("th", "hw") else T[a[0]][:]
+        if not isinstance(a, dict):
+            return a
+        if "win" in a:
+            return ap(a["win"]).indirect(ap(a["off"]))
+        cols = slice(a["lo"], a["hi"], a["st"]) if a["st"] > 1 else slice(a["lo"], a["hi"])
+        return T[a["n"]][slice(*a["p"]) if a["p"] else slice(None), cols]
+
+    def engines(src):
+        both = -1
+        for other in T.cores:
+            if other != src:
+                both &= topo.mask(src, other)
+        return both
+    mark, count, know, clock, total = {}, {}, {e: {} for e in Q}, {}, {}
+    nd = [0]
+    for i in order:
+        o = L[i]
+        e, k, a = o["e"], o["k"], o["a"]
+        if k == "arrive":
+            src = T.cores[(rank - L[o["peer"]]["a"][3]) % N]
+            mark[i] = (a[1], bin(engines(src)).count("1"))
+            clock[i] = {}
+            total[a[1]] = mark[i][1]
+            continue
+        q, kn = Q[e], know[e]
+        for j in sorted(o["deps"], key=lambda j: -mark[j][1]):
+            if e == "T" and L[j]["e"] == "T":
+                continue
+            s, n = mark[j]
+            if kn.get(s, 0) < n:
+                q.wait_ge(T.sem[s], n)
+                kn[s] = n
+                for s2, n2 in clock[j].items():
+                    kn[s2] = max(kn.get(s2, 0), n2)
+        clock[i] = dict(kn)
+        x = [ap(z) for z in a]
+        if k == "dma":
+            s = "d%d" % nd[0]
+            nd[0] += 1
+            q.dma_start(x[0], x[1]).then_inc(T.sem[s], 16)
+            mark[i] = (s, 16)
+            total[s] = 16
+            continue
+        if k == "send":
+            dst, m = T.cores[(rank + a[3]) % N], engines(core)
+            g.remote_dma(x[0], x[1], T.sem[a[2]], T.sem.lo, topo.addr(dst)[1], topo.addr(dst)[0], m)
+            total["lo"] = total.get("lo", 0) + bin(m).count("1")
+            mark[i] = ("lo", total["lo"])
+            continue
+        if k == "ts":
+            ins = q.tensor_scalar(x[0], x[1], x[2], None, x[3]) if x[5] is None else q.tensor_scalar(x[0], x[1], x[2], x[4], x[3], x[5])
+        elif k == "tt":
+            ins = q.tensor_tensor(x[0], x[1], x[2], x[3])
+        elif k == "cp":
+            ins = q.tensor_copy(x[0], x[1])
+        elif k == "set":
+            ins = q.memset(x[0], x[1])
+        elif k == "scan":
+            ins = q.tensor_tensor_scan(x[0], x[1], x[2], 0.0, x[3], x[4])
+        elif k == "red":
+            ins = q.tensor_reduce(x[0], x[1], AX.X, OP.add)
+        elif k == "act":
+            ins = q.activation(x[0], x[1], x[2], bias=x[3], scale=x[4], accum_out=x[5])
+        elif k == "mm":
+            ins = q.matmul(x[0], x[1], x[2], x[3], x[4])
+        elif k == "iota":
+            if SB[a[0]["n"]][1] == i32:
+                ins = g.iota(x[0], x[1], x[2], x[3])
+            else:
+                ins = g.iota(x[0], x[1], x[2], x[3], allow_small_or_imprecise_dtypes=True)
+        else:
+            ins = g.affine_select(x[0], x[1], [[0, P]], OP.is_ge, 0.0, 0, 0)
+        count[e] = count.get(e, 0) + 1
+        ins.then_inc(T.sem[e], 1)
+        mark[i] = (e, count[e])
+        total[e] = count[e]
+    for s, n in total.items():
+        g.wait_ge(T.sem[s], n)

@@ -1,4 +1,5 @@
-from concourse.mybir import AluOpType as OP, AxisListType as AX, ActivationFunctionType as AF
+import numpy
+from concourse.mybir import AluOpType as OP, ActivationFunctionType as AF
 
 N, M, P, NT, E = 8, 2304, 256, 4, 3328
 DUM = 3336
@@ -7,40 +8,37 @@ XW = 320
 SW = 304
 BIG, FRZ = float(1 << 22), float(1 << 21)
 CH = 64
-MODES = ["BBRRRRRRLLLL"]
-CFG = {"split": 2, "prem": 2000.0}
-ROUNDS = 3
+MODES = ["BBRBBRARAALA", "BRRBBRARAALA", "BRRBBRARAALA", "BRRBBRARAALA"]
+TRIES = 2100
+BIAS = {"Vxrep": 3000.0, "Vs2": -500.0, "TPM": 300.0, "VA": 1500.0, "Vm4": 300.0, "SG": 1500.0, "Vdlt": 800.0, "Sjk": 3000.0,
+        "Vs3": 800.0}
 
 f32, b16, i32, u16 = "float32", "bfloat16", "int32", "uint16"
 SB = {
     "PT": (M, i32), "A": (AW, f32), "F": (3336, b16), "XS": (NT * XW, b16), "xrep": (NT * 4096, b16),
     "thi": (4, i32), "hwi": (4, i32), "pi": (4, i32), "ri": (4, i32), "K": (40, f32),
-    "J": (256, f32), "JG": (128, f32), "JR": (128, f32), "NA": (1024, f32), "NK": (1088, f32), "EN": (1024, f32),
+    "J": (256, f32), "JG": (128, f32), "JR": (128, f32), "NA": (1024, f32), "NK": (1088, f32),
     "CW": (256, f32), "CT": (256, f32), "CK": (768, f32), "TA": (768, b16), "TB": (768, b16), "PW": (48, f32), "DP": (48, f32),
-    "SO": (48, u16), "ONE": (SW, b16),
-    "Sel": (144, b16), "Sel2": (144, b16), "Seln": (144, b16), "I": (128, b16), "In": (128, b16), "BO": (128, b16),
-    "BOf": (128, f32), "S0f": (128, f32), "S0b": (128, b16), "S0n": (128, b16), "S0h": (128, b16), "BOw": (128, b16),
-    "BOk": (128, b16), "BO4": (128, b16), "HS": (128, b16), "HS2": (128, b16), "S0k": (128, b16), "ZT": (128, b16),
-    "ZTh": (128, b16), "TriF": (128, b16),
-    "Ir": (128, b16), "m1": (128, b16), "m2": (128, b16), "m3": (128, b16), "m4": (128, b16), "m5": (128, b16),
+    "ONE": (SW, b16), "Sel": (144, b16), "Sel2": (144, b16), "Seln": (144, b16), "BOf": (128, f32), "S0f": (128, f32),
     "scn": (768, f32), "kw": (48, u16), "ki": (48, i32), "lo": (48, i32), "ow": (48, u16), "s1": (48, f32), "s2": (48, f32),
     "s3": (48, f32), "sc": (48, u16), "cb": (832, f32), "cu": (768, u16), "fs": (1024, b16), "cval": (768, f32),
-    "d": (4 * 1024, b16), "ad": (4 * 1024, b16), "G": (4096, b16), "Gs": (2048, b16), "ab": (1024, b16), "sg": (3 * SW, b16),
-    "xc": (P, b16), "d0": (768, b16), "a0": (768, b16), "r0": (768, b16), "okn": (768, b16), "e": (768, b16), "gs": (768, b16),
-    "Kw": (2 * XW, f32), "y": (768, f32), "dlt": (768, f32),
+    "d": (4096, b16), "ad": (4096, b16), "G": (4096, b16), "Gs": (2048, b16), "ab": (1024, b16), "sg": (3 * SW, b16),
+    "xc": (P, b16), "Kw": (2 * XW, f32), "y": (768, f32), "dlt": (768, f32),
     "esc": (SW, b16), "cnt": (SW, b16), "jk": (3 * SW, b16), "acc": (4, f32), "pl": (4, u16),
-    "msg": (3 * 48, b16), "req": (3 * 48, b16), "out": (3 * 48, b16), "rep": (3 * 48, b16),
-    "qs": (48, f32), "qi": (4, i32), "qj": (4, i32), "qw": (4, u16), "cq": (48, u16), "xq": (768, b16), "dq": (768, b16),
-    "aq": (768, b16), "ks": (768, f32), "bi": (4, i32), "bj": (4, i32), "bw": (4, u16),
-    "xo": (48, f32), "xs": (48, b16), "xn": (144, b16), "cua": (144, u16), "Ga": (2304, b16), "sga": (144, b16),
+    "qs": (48, f32), "qi": (4, i32), "qj": (4, i32), "qw": (4, u16), "cq": (48, u16),
+    "ks": (768, f32), "bi": (4, i32), "bj": (4, i32), "bw": (4, u16),
+    "xo": (48, f32), "xs": (48, b16), "cua": (144, u16), "Ga": (2304, b16),
 }
+SB.update({k: (128, b16) for k in "I In BO S0b S0n S0h BOw BOk HN HS HS2 S0k ZTh TriF CW1 Ir m1 m2 m3 m4 m5 m6 rt".split()})
+SB.update({k: (768, b16) for k in "d0 a0 r0 okn e gs Rn dq aq".split()})
+SB.update({k: (144, b16) for k in "msg req out rep xn sga".split()})
 PS = {"PB": 2048, "PD": 1024, "PM": 1024}
 SCRATCH = {k: ("sbuf", [128, w], t) for k, (w, t) in SB.items()}
 SCRATCH.update({k: ("psum", [128, w], f32) for k, w in PS.items()})
 SEMAPHORES = ["V", "S", "T", "G", "lo"] + ["q%d" % t for t in range(3)] + ["a%d" % t for t in range(3)] + ["d%d" % i for i in range(40)]
 
-(RF, GB, PF, G15, M0, N0M, M1E, OFW, OF7, TH, BSG, R0S, R0B, FB0, FB1, FB2, FB3, BZ1, BZ2, BZ3, BW, LB, SL0, SL1, SL2,
- NKB, HW, HSC, RP1, T1, T2, T3, T4, T5, T6, T7) = range(36)
+(RF, GB, PF, G15, M0, N0M, M1E, OFW, OF7, TH, BSG, R0S, R0B, FB0, FB1, FB2, FB3, BZ1, BZ2, BZ3, LB, SL0, SL1, SL2,
+ NKB, HW, HSC, RP1, T1, T2, T3, T4, T5, T6) = range(34)
 
 
 def v(n, lo=0, hi=None, st=1, p=None):
@@ -61,39 +59,37 @@ def size(a):
     return 4 if a["n"] in PS or SB[a["n"]][1] in (f32, i32) else 2
 
 
-REF = {"cyc": 1.04, "g": 1.56, "s": 3.8, "pe": 0.52, "lat": 110.0, "rem": 4000.0, "dma": 2200.0, "bw": 100.0, "tt": 2.0}
-OTHERS = [{}, {"g": 1.15, "s": 2.2}, {"g": 2.0, "s": 5.5}, {"pe": 0.7}, {"rem": 7000.0, "lat": 200.0}]
+REF = {"cyc": 1.0, "g": 1.8, "s": 4.3, "pe": 0.5, "lat": 110.0, "rem": 3500.0, "dma": 2200.0, "bw": 180.0, "first": 3000.0}
+OTHERS = [{"cyc": 0.83, "pe": 0.42, "g": 1.56, "s": 3.8, "rem": 2500.0, "bw": 200.0, "dma": 1500.0, "lat": 100.0},
+          {"cyc": 1.2, "pe": 0.6, "g": 1.9, "s": 5.0, "rem": 3500.0, "bw": 150.0, "lat": 110.0},
+          {"cyc": 1.1, "pe": 0.56, "g": 2.08, "s": 6.0, "rem": 3000.0, "lat": 80.0},
+          {"cyc": 0.95, "pe": 0.48, "g": 2.0, "s": 2.0, "rem": 4000.0, "lat": 160.0},
+          {"cyc": 0.9, "pe": 0.45, "g": 1.4, "s": 4.5, "rem": 5500.0, "lat": 130.0, "first": 5000.0}]
 
 
 def cost(o, c):
     k, a = o["k"], o["a"]
-    if k == "dma":
-        return 60.0
-    if k in ("send", "arrive"):
-        return 500.0 if k == "send" else 0.0
+    if k in ("dma", "send", "arrive"):
+        return {"dma": 60.0, "send": 500.0, "arrive": 0.0}[k]
     if k == "mm":
         return max(64, a[2]["w"]) * c["pe"] * (4 if size(a[2]) == 4 else 1) + 10
     w = a[0]["w"]
-    if k == "iota":
-        return 130 + 2 * w * c["cyc"]
-    if k == "sel":
-        return 170 + 2 * w * c["cyc"]
+    if k in ("iota", "sel"):
+        return (130 if k == "iota" else 170) + 2 * w * c["cyc"]
     if "win" in a[0]:
         return 50 + c["s"] * w * c["cyc"]
     if k != "set" and "win" in a[1]:
         return 60 + c["g"] * w * c["cyc"]
     if k == "act":
         return 65 + max(64, w) * c["cyc"]
-    if k == "red":
-        return 40 + max(64, a[1]["w"]) * c["cyc"]
     aps = [x for x in a if isinstance(x, dict) and x["w"] == w]
     f = 0.5 if all(size(x) == 2 for x in aps) else 1.0
     if k == "tt":
-        f = 1.0 if any(x["n"] in PS for x in aps[1:]) else c["tt"]
+        f = 1.0 if any(x["n"] in PS for x in aps[1:]) else 2.0
     return 40 + max(64, w * f) * c["cyc"]
 
 
-def program(modes):
+def program(allm):
     L = []
 
     def op(eng, k, *a):
@@ -112,12 +108,11 @@ def program(modes):
     def iota(out, pat, base, cm): op("G", "iota", out, pat, base, cm)
     def dma(q, out, x, nbytes, after=None): op(q, "dma", out, x, nbytes, after)
     ID = AF.Identity
-    nh = 2 if modes[8:] == "LLLL" else 3
 
     dma("Q", v("PT", 2048, M), ("ptr", 2048, M), 128 * 1024)
     dma("S", v("F", M, M + P), ("nw", 0, P), 128 * 512)
-    dma("Q", v("PT", 0, 1024), ("ptr", 0, 1024), 128 * 4096)
-    dma("S", v("PT", 1024, 2048), ("ptr", 1024, 2048), 128 * 4096)
+    for i in range(4):
+        dma("QS"[i % 2], v("PT", 512 * i, 512 * i + 512), ("ptr", 512 * i, 512 * i + 512), 128 * 2048 * (i // 2 + 1))
     dma("Q", v("F", 0, M), ("fr", 0, M), 128 * 4608)
     dma("S", v("F", M + P, E), ("nw", P, 1024), 128 * 1536)
     iota(v("pi", 0, 1), [[0, 1]], 0, 1)
@@ -170,13 +165,12 @@ def program(modes):
     act(kc(R0B), kc(T1), ID, scale=-1.0, bias=kc(M0))
     for t in range(NT):
         act(kc(FB0 + t), kc(M0), ID, scale=float(E - (M + P * t - P)), bias=0.5 - E)
-    act(kc(T2), kc(RF), ID, scale=-0.5, bias=1.0)
+    act(kc(T2), kc(RF), ID, scale=-1.0, bias=2.0)
     act(kc(BZ1), kc(M0), ID, scale=-200.0, bias=kc(T2))
     act(kc(BZ2), kc(BZ1), ID, bias=-2048.0)
-    act(kc(T4), kc(M0), ID, scale=-7.5, bias=kc(T2))
+    act(kc(T4), kc(M0), ID, scale=-16.0, bias=kc(T2))
     act(kc(BZ3), kc(T4), ID, bias=-2048.0)
-    act(kc(T5), kc(RF), ID, scale=-2048.0, bias=-4096.0 * 6.5)
-    act(kc(BW), kc(M0), ID, scale=-1.0e6, bias=kc(T5))
+    act(kc(T5), kc(M0), ID, scale=-30720.0 - 2048.0, bias=2048.0)
     act(kc(LB), kc(N0M), ID, scale=float(E))
     for b in range(3):
         act(kc(SL0 + b), kc(RF), ID, bias=16.0 * b + 0.5)
@@ -185,13 +179,13 @@ def program(modes):
     act(kc(T6), kc(M0), ID, scale=30720.0, bias=2048.0)
     act(v("NK", 0, 1024), v("NA"), ID, scale=kc(N0M), bias=kc(NKB))
     mset(v("NK", 1024, 1088), 4000.0)
-    iota(v("EN"), [[-1, 1024]], E - M, 0)
     iota(v("TA"), [[16, 48], [0, 16]], 0, 0)
     iota(v("TB"), [[0, 48], [1, 16]], 0, 0)
     mset(v("TB", 0, 768, 16), 1.75 * (1 << 20))
     ts(v("PW"), v("PW"), kc(RF), OP.add)
     act(v("DP"), v("PW"), ID, bias=float(DUM + 768))
-    cp(v("SO"), v("J", 0, 48))
+    act(kc(T3), kc(PF), ID, scale=16.0)
+    ts(v("Rn"), v("TA"), kc(T3), OP.is_equal, -1.0, OP.mult)
     mset(v("ONE"), 1.0)
     mset(v("cb", 768, 832), 0.0)
     mset(v("esc", P, SW), 1.0)
@@ -202,26 +196,30 @@ def program(modes):
     for t in range(NT):
         mset(v("XS", XW * t + P, XW * t + SW), 0.0)
         mset(v("XS", XW * t + SW, XW * t + XW), 99.0)
-    for name, sc_ in (("BOf", 1.0), ("S0b", kc(M0)), ("BOw", kc(HW)), ("BOk", 1024.0), ("BO4", 4096.0), ("HS", kc(HSC)),
+    for name, sc_ in (("BOf", 1.0), ("S0b", kc(M0)), ("BOw", kc(HW)), ("BOk", 1024.0), ("HN", kc(T5)), ("HS", kc(HSC)),
                       ("HS2", kc(T6))):
         act(v(name), v("BO"), ID, scale=sc_)
-    act(v("S0n"), v("S0b"), ID, scale=-1.0)
-    act(v("S0h"), v("S0b"), ID, scale=-0.5)
+    act(v("S0n"), v("S0b"), ID, scale=-8192.0)
+    act(v("S0h"), v("S0b"), ID, scale=-4096.0)
     act(v("S0k"), v("S0b"), ID, scale=-2048.0)
     ts(v("m1"), v("JR"), kc(RF), OP.is_gt, kc(N0M), OP.mult)
     tt(v("m1"), v("m1"), v("BO"), OP.mult)
     act(v("m2"), v("I"), ID, scale=kc(N0M))
     act(v("m3"), v("m2"), ID, scale=-16.0)
     tt(v("m3"), v("m3"), v("m1"), OP.add)
-    act(v("TriF"), v("m3"), ID, scale=0.5)
+    act(v("TriF"), v("m3"), ID, scale=4096.0)
     ts(v("m4"), v("JR"), 0.0, OP.is_equal, kc(N0M), OP.mult)
     tt(v("m4"), v("m4"), v("BO"), OP.mult)
     tt(v("m4"), v("m4"), v("m1"), OP.add)
-    tt(v("ZT"), v("m4"), v("m2"), OP.subtract)
-    act(v("ZTh"), v("ZT"), ID, scale=0.5)
+    tt(v("m4"), v("m4"), v("m2"), OP.subtract)
+    act(v("ZTh"), v("m4"), ID, scale=0.5)
     act(v("m5"), v("JR"), ID, scale=0.5, bias=7.0)
     tt(v("m5"), v("m5"), v("S0b"), OP.mult)
-    tt(v("Ir"), v("m5"), v("m2"), OP.add)
+    tt(v("m6"), v("m5"), v("m2"), OP.add)
+    act(v("Ir"), v("m6"), ID, scale=8192.0)
+    ts(v("m6"), v("S0b"), 0.5, OP.mult)
+    tt(v("m6"), v("m6"), v("m5"), OP.add)
+    act(v("CW1"), v("m6"), ID, scale=8192.0)
 
     def sel(n, i): return v(n, 15 - i, 143 - i)
     def blk(n, h, w=P): return v(n, w * h, w * h + P)
@@ -249,8 +247,10 @@ def program(modes):
     link = bank("PB", 3)
     grp(link, [(v("S0f"), v("A", 2048, M))])
     nd = [0, 0]
+    nh = 3
     for t in range(NT):
         n0 = M + P * t
+        modes = allm[t]
         X = v("XS", XW * t, XW * t + XW)
         x = v("XS", XW * t, XW * t + P)
         prev = v("A", n0 - P, n0)
@@ -280,6 +280,9 @@ def program(modes):
             rq = v("req", 48 * t - 48, 48 * t)
             op("X", "arrive", rq, "q%d" % (t - 1))
             qp = v("PM", 0, 48)
+            tp, rt = v("PM", 512, 640, 1, (0, 48)), v("rt", 0, 128, 1, (0, 48))
+            grp(tp, [(rq, v("I"))])
+            act(rt, tp, ID)
             grp(qp, [(v("BOw"), rq)])
             scan(v("qs"), v("CW", 0, 48), qp, OP.add, OP.min)
             ts(v("qi", 0, 3), v("qs", 15, 48, 16), kc(OFW), OP.add)
@@ -287,16 +290,16 @@ def program(modes):
             cp(v("qw", 0, 3), v("qj", 0, 3))
             cp(v("cq"), ind(v("A", 0, 2048), v("qw", 0, 3)))
             for lo, hi in ((0, 512), (512, 768)):
-                act(v("xq", lo, hi), ind(rq, v("SO", lo // 16, hi // 16)), ID)
-                tt(v("dq", lo, hi), ind(FG, v("cq", lo // 16, hi // 16)), v("xq", lo, hi), OP.subtract)
-                act(v("aq", lo, hi), v("dq", lo, hi), AF.Abs)
+                act(v("dq", lo, hi), ind(FG, v("cq", lo // 16, hi // 16)), ID)
+                grp(v("PM", lo, hi), [(rt, v("Rn", lo, hi, 1, (0, 48))), (v("I"), v("dq", lo, hi))])
+                act(v("aq", lo, hi), v("PM", lo, hi), AF.Abs)
                 grp(v("PM", lo, hi), [(v("S0b"), v("TA", lo, hi)), (v("S0b"), v("TB", lo, hi)), (v("BOk"), v("aq", lo, hi))])
                 scan(v("ks", lo, hi), v("CK", lo, hi), v("PM", lo, hi), OP.add, OP.min)
             ts(v("bi", 0, 3), v("ks", 255, 768, 256), kc(OFW), OP.add)
             ts(v("bj", 0, 3), v("bi", 0, 3), 1023, OP.bitwise_and)
             cp(v("bw", 0, 3), v("bj", 0, 3))
             ro = v("out", 48 * t - 48, 48 * t)
-            tt(ro, ind(v("dq"), v("bw", 0, 3)), rq, OP.add)
+            cp(ro, ind(v("dq"), v("bw", 0, 3)))
             op("G", "send", v("rep", 48 * t - 48, 48 * t), ro, "a%d" % (t - 1), -(1 + (t - 1) % (N - 1)))
             pl = v("pl", 0, 3)
             ts(v("xo"), ind(X, pl), 383.5, OP.add)
@@ -326,10 +329,9 @@ def program(modes):
                 o = 1024 * (nd[0] % 4)
                 nd[0] += 1
                 d, ad = v("d", o, o + 16 * CH), v("ad", o, o + 16 * CH)
-                w = CH // CFG["split"]
-                for u in range(0, CH, w):
-                    tt(v("d", o + 16 * u, o + 16 * (u + w)), ind(FG, v("cu", P * h + s0 + u, P * h + s0 + u + w)),
-                       v("xrep", 4096 * t + 16 * (s0 + u), 4096 * t + 16 * (s0 + u + w)), OP.subtract)
+                for u in (0, 32):
+                    tt(v("d", o + 16 * u, o + 16 * u + 512), ind(FG, v("cu", P * h + s0 + u, P * h + s0 + u + 32)),
+                       v("xrep", 4096 * t + 16 * (s0 + u), 4096 * t + 16 * (s0 + u) + 512), OP.subtract)
                 if mode == "A":
                     act(ad, d, AF.Abs)
                     grp(dout, [(sel("Sel", i), v("ad", o + i, o + 16 * CH, 16)) for i in range(1, 16)])
@@ -347,8 +349,8 @@ def program(modes):
                 ts(v("xn", 48 * h, 48 * h + 48), v("xs"), 0.5, OP.mult, -192.0, OP.add)
             cp(ind(X, pl), v("xn", 0, 48))
             da = v("PB", 1536, 1536 + 48 * nh)
-            by_pe("Ga", 0, 48 * nh, v("xn", 0, 48 * nh), da)
-            act(v("sga", 0, 48 * nh), da, AF.Sign, bias=kc(BSG), scale=-1.0)
+            by_pe("Ga", 0, 48 * nh, v("xn"), da)
+            act(v("sga"), da, AF.Sign, bias=kc(BSG), scale=-1.0)
             for h in range(2):
                 cp(ind(v("sg", SW * h, SW * h + SW), pl), v("sga", 48 * h, 48 * h + 48))
         dma("Q", ("yx", P * t, P * t + P), x, 128 * 512)
@@ -362,7 +364,7 @@ def program(modes):
             by_pe("G", 16 * s0, CH, v("XS", XW * t + s0, XW * t + s0 + CH), dout)
         if late:
             act(blk("sg", 2, SW), dh[2], AF.Sign, bias=kc(BSG), scale=-1.0)
-        if t > 0 and nh == 3:
+        if t > 0:
             cp(ind(v("sg", SW * 2, SW * 3), pl), v("sga", 96, 144))
         if t + 1 < NT:
             cp(v("F", n0, n0 + P), x)
@@ -375,9 +377,9 @@ def program(modes):
             col = [(v("TriF"), blk("fs", h + 1)), (v("S0h"), blk("fs", h))]
             wr = [(v("S0n"), blk("e", j)) for j in es[h]]
             grp(U[h], col + [(v("Ir"), blk("r0", h))] + wr)
-            ts(blk("okn", h), U[h], -0.5, OP.is_lt)
+            act(blk("okn", h), U[h], AF.Sign, bias=-0.5, scale=-1.0)
             old = [(v("S0k"), blk("gs", h - 1))] if h else []
-            grp(H[h], old + [(v("HS2" if h else "HS"), blk("sg", h, SW)), (v("BO4"), blk("okn", h))])
+            grp(H[h], old + [(v("HS2" if h else "HS"), blk("sg", h, SW)), (v("HN"), blk("okn", h))])
             if h < 2:
                 kwin = v("Kw", XW * h, XW * h + XW)
                 tt(blk("Kw", h, XW), H[h], prev if h == 0 else blk("cb", 0), OP.add)
@@ -385,25 +387,21 @@ def program(modes):
                     tt(blk("e", 0), ind(kwin, ow(1)), blk("cb", 0), OP.is_equal)
                 tt(blk("e", 1 + h), ind(kwin, ow(2)), blk("cb", 1), OP.is_equal)
             elif t + 1 < NT:
-                ts(v("esc", 0, P), H[2], 0.5, OP.is_lt)
+                act(v("esc", 0, P), H[2], AF.Relu, bias=1.0, scale=-1.0)
                 scan(v("cnt"), v("ONE"), v("esc"), OP.mult, OP.add)
-                for b in range(2):
+                for b in range(3):
                     act(v("jk", SW * b, SW * b + SW), v("cnt"), AF.Sign, bias=kc(SL0 + b), scale=-1.0, acc=v("acc", b, b + 1))
-                ts(v("jk", 2 * SW, 3 * SW), v("cnt"), kc(SL2), OP.is_le, 2.0, OP.mult)
-                op("V", "red", kc(T7), v("jk", 2 * SW, 3 * SW))
-                ts(v("acc", 2, 3), kc(T7), -float(SW), OP.add)
                 ts(v("pl", 0, 3), v("acc", 0, 3), 0.5, OP.mult, SW / 2.0, OP.add)
                 ms = v("msg", 48 * t, 48 * t + 48)
                 cp(ms, ind(X, v("pl", 0, 3)))
                 op("G", "send", v("req", 48 * t, 48 * t + 48), ms, "q%d" % t, 1 + t % (N - 1))
             act(blk("gs", h), H[h], AF.Sign, bias=0.5, scale=-1.0)
-            grp(Z[h], old + [(v("ZTh"), blk("sg", h, SW)), (v("ZT"), blk("okn", h))])
+            grp(Z[h], old + [(v("ZTh"), blk("sg", h, SW)), (v("ZTh"), blk("okn", h))])
             act(Z[h], Z[h], AF.Relu, bias=kc(BZ1 + h), scale=-1.0)
             tt(blk("y", h), Z[h], blk("cval", h), OP.mult)
-            grp(W[h], col + wr + [(v("S0h"), blk("gs", h))])
-            act(W[h], W[h], AF.Relu, bias=kc(BW), scale=-4096.0)
-            tt(blk("dlt", h), W[h], blk("EN", t), OP.min)
-            tt(ind(v("A"), v("sc", 16 * h, 16 * h + 16)), blk("cb", h), blk("dlt", h), OP.subtract)
+            grp(W[h], col + [(v("CW1"), blk("r0", h))] + wr + [(v("S0h"), blk("gs", h))])
+            tt(blk("dlt", h), W[h], blk("cb", h), OP.min)
+            tt(ind(v("A"), v("sc", 16 * h, 16 * h + 16)), blk("dlt", h), blk("cval", h), OP.max)
         grp(link, [(v("BOf"), blk("y", h)) for h in range(3)])
     act(v("A", E - P, E), link, ID, scale=kc(M0), bias=kc(LB))
     for q, lo, hi in (("Q", 0, 1536), ("S", 1536, 3072), ("Q", 3072, E)):
@@ -457,25 +455,36 @@ def depend(L):
             sent[o["a"][2]] = i
         o["deps"] = sorted(deps)
         o["peer"] = sent[o["a"][1]] if o["k"] == "arrive" else None
+        a = o["a"][0]
+        o["keys"] = (o["e"] + a["n"], (o["e"], a["n"], a.get("lo"))) if isinstance(a, dict) else ("", "")
     return L
 
 
-def schedule(L, c, fixed, rounds=0):
-    n = len(L)
+def tables(L, c):
     dur = [cost(o, c) for o in L]
     late = [c["dma"] + o["a"][2] / c["bw"] if o["k"] == "dma" else 0.0 for o in L]
     pre, suc = [], [[] for _ in L]
     for i, o in enumerate(L):
-        pre.append([(j, 0.0 if o["e"] == "T" and L[j]["e"] == "T" else c["lat"] + late[j]) for j in o["deps"]]
-                   + ([(o["peer"], c["rem"])] if o["peer"] is not None else []))
+        pre.append([(j, 0.0 if o["e"] == "T" and L[j]["e"] == "T" else c["lat"] + late[j]) for j in o["deps"]])
+        if o["peer"] is not None:
+            pre[i].append((o["peer"], c["rem"] + (c["first"] if o["a"][1] == "q0" else 0.0)))
         for j, w in pre[i]:
             suc[j].append((i, w))
-    if fixed is not None:
-        fin, free = [0.0] * n, {}
-        for i in fixed:
-            st = max([free.get(L[i]["e"], 0.0)] + [fin[j] + w for j, w in pre[i]])
-            fin[i] = free[L[i]["e"]] = st + dur[i]
-        return fin, max(fin[i] + late[i] for i in range(n))
+    return dur, late, pre, suc
+
+
+def replay(L, tab, order):
+    dur, late, pre = tab[:3]
+    fin, free = [0.0] * len(L), {}
+    for i in order:
+        st = max([free.get(L[i]["e"], 0.0)] + [fin[j] + w for j, w in pre[i]])
+        fin[i] = free[L[i]["e"]] = st + dur[i]
+    return max(fin[i] + late[i] for i in range(len(L)))
+
+
+def schedule(L, tab, bias):
+    n = len(L)
+    dur, late, pre, suc = tab
 
     def place(seq, before, head):
         busy, fin = {}, [0.0] * n
@@ -491,27 +500,43 @@ def schedule(L, c, fixed, rounds=0):
             slots.insert(at, (st, st + dur[i]))
             fin[i] = st + dur[i]
         return fin
-    prio = [dur[i] + late[i] + 0.001 for i in range(n)]
+    more = [max(0.0, dur[i] + bias.get(o["keys"][0], 0.0) + bias.get(o["keys"][1], 0.0)) for i, o in enumerate(L)]
+    prio = [more[i] + late[i] + 0.001 for i in range(n)]
     for i in range(n - 1, -1, -1):
         for j, w in pre[i]:
-            prio[j] = max(prio[j], dur[j] + (CFG["prem"] if L[i]["peer"] == j else w) + prio[i] + 0.001)
+            prio[j] = max(prio[j], more[j] + (1000.0 if L[i]["peer"] == j else w) + prio[i] + 0.001)
     res = []
-    for r in range(rounds + 1):
+    for r in range(2):
         fin = place(sorted(range(n), key=lambda i: (-prio[i], i)), pre, [0.0] * n)
         res.append(sorted(range(n), key=lambda i: (fin[i] - dur[i], fin[i], i)))
-        prio = place(sorted(range(n), key=lambda i: (-fin[i], dur[i] - fin[i], -i)), suc, late)
+        if r == 0:
+            prio = place(sorted(range(n), key=lambda i: (-fin[i], dur[i] - fin[i], -i)), suc, late)
     return res
 
 
 def plan():
-    best = None
-    for modes in MODES:
-        L = depend(program(modes))
-        for r, order in enumerate(schedule(L, REF, None, ROUNDS)):
-            end = sum(schedule(L, dict(REF, **c), order)[1] for c in OTHERS) / len(OTHERS)
-            if best is None or end < best[2]:
-                best = (L, order, end, modes, r)
-    return best
+    L = depend(program(MODES))
+    ref, tabs = tables(L, REF), [tables(L, dict(REF, **c)) for c in OTHERS]
+    keys = sorted({o["keys"][1] for o in L if o["e"] in "VST" and o["keys"][0] and o["keys"][1][1] not in ("xrep", "K")}, key=str)
+    unit = [replay(L, tab, schedule(L, ref, BIAS)[1]) for tab in tabs]
+
+    def score(bias):
+        res = []
+        for order in schedule(L, ref, bias):
+            e = [replay(L, tab, order) / u for tab, u in zip(tabs, unit)]
+            res.append((max(e) + sum(e) / len(e), order))
+        return min(res)
+    rs = numpy.random.RandomState(1)
+    bias = dict(BIAS)
+    best = score(bias)
+    for _ in range(TRIES):
+        new = dict(bias)
+        for _ in range(int(rs.randint(1, 4))):
+            new[keys[int(rs.randint(len(keys)))]] = (-500.0, 0.0, 300.0, 800.0, 1500.0, 3000.0)[int(rs.randint(6))]
+        got = score(new)
+        if got[0] <= best[0]:
+            best, bias = got, new
+    return L, best[1], best[0]
 
 
 PLAN = []
@@ -588,8 +613,6 @@ def rank_program(g, core, T, topo):
             ins = q.memset(x[0], x[1])
         elif k == "scan":
             ins = q.tensor_tensor_scan(x[0], x[1], x[2], 0.0, x[3], x[4])
-        elif k == "red":
-            ins = q.tensor_reduce(x[0], x[1], AX.X, OP.add)
         elif k == "act":
             ins = q.activation(x[0], x[1], x[2], bias=x[3], scale=x[4], accum_out=x[5])
         elif k == "mm":

import numpy
from concourse.mybir import AluOpType as OP, ActivationFunctionType as AF

N, M, P, NT, E = 8, 2304, 256, 4, 3328
DUM = 3336
AW = DUM + P
XW = 320
SW = 304
BIG, FRZ = float(1 << 22), float(1 << 21)
CH = 64
MODES = ["BBRBBRARAALA", "BRRBBRARAALA", "BRRBBRARAALA", "BRRBBRARAALA"]
TRIES = 2100
BIAS = {"Vxrep": 3000.0, "Vs2": -500.0, "TPM": 300.0, "VA": 1500.0, "Vm4": 300.0, "SG": 1500.0, "Vdlt": 800.0, "Sjk": 3000.0,
        "Vs3": 800.0}

f32, b16, i32, u16 = "float32", "bfloat16", "int32", "uint16"
SB = {
    "PT": (M, i32), "A": (AW, f32), "F": (3336, b16), "XS": (NT * XW, b16), "xrep": (NT * 4096, b16),
    "thi": (4, i32), "hwi": (4, i32), "pi": (4, i32), "ri": (4, i32), "K": (40, f32),
    "J": (256, f32), "JG": (128, f32), "JR": (128, f32), "NA": (1024, f32), "NK": (1088, f32),
    "CW": (256, f32), "CT": (256, f32), "CK": (768, f32), "TA": (768, b16), "TB": (768, b16), "PW": (48, f32), "DP": (48, f32),
    "ONE": (SW, b16), "Sel": (144, b16), "Sel2": (144, b16), "Seln": (144, b16), "BOf": (128, f32), "S0f": (128, f32),
    "scn": (768, f32), "kw": (48, u16), "ki": (48, i32), "lo": (48, i32), "ow": (48, u16), "s1": (48, f32), "s2": (48, f32),
    "s3": (48, f32), "sc": (48, u16), "cb": (832, f32), "cu": (768, u16), "fs": (1024, b16), "cval": (768, f32),
    "d": (4096, b16), "ad": (4096, b16), "G": (4096, b16), "Gs": (2048, b16), "ab": (1024, b16), "sg": (3 * SW, b16),
    "xc": (P, b16), "Kw": (2 * XW, f32), "y": (768, f32), "dlt": (768, f32),
    "esc": (SW, b16), "cnt": (SW, b16), "jk": (3 * SW, b16), "acc": (4, f32), "pl": (4, u16),
    "qs": (48, f32), "qi": (4, i32), "qj": (4, i32), "qw": (4, u16), "cq": (48, u16),
    "ks": (768, f32), "bi": (4, i32), "bj": (4, i32), "bw": (4, u16),
    "xo": (48, f32), "xs": (48, b16), "cua": (144, u16), "Ga": (2304, b16),
}
SB.update({k: (128, b16) for k in "I In BO S0b S0n S0h BOw BOk HN HS HS2 S0k ZTh TriF CW1 Ir m1 m2 m3 m4 m5 m6 rt".split()})
SB.update({k: (768, b16) for k in "d0 a0 r0 okn e gs Rn dq aq".split()})
SB.update({k: (144, b16) for k in "msg req out rep xn sga".split()})
PS = {"PB": 2048, "PD": 1024, "PM": 1024}
SCRATCH = {k: ("sbuf", [128, w], t) for k, (w, t) in SB.items()}
SCRATCH.update({k: ("psum", [128, w], f32) for k, w in PS.items()})
SEMAPHORES = ["V", "S", "T", "G", "lo"] + ["q%d" % t for t in range(3)] + ["a%d" % t for t in range(3)] + ["d%d" % i for i in range(40)]

(RF, GB, PF, G15, M0, N0M, M1E, OFW, OF7, TH, BSG, R0S, R0B, FB0, FB1, FB2, FB3, BZ1, BZ2, BZ3, LB, SL0, SL1, SL2,
 NKB, HW, HSC, RP1, T1, T2, T3, T4, T5, T6) = range(34)


def v(n, lo=0, hi=None, st=1, p=None):
    if hi is None:
        hi = (SB[n][0] if n in SB else PS[n])
    return {"n": n, "lo": lo, "hi": hi, "st": st, "p": p, "w": len(range(lo, hi, st))}


def kc(c):
    return v("K", c, c + 1)


def ind(win, off):
    return {"win": win, "off": off, "w": 16 * off["w"], "n": win["n"]}


def size(a):
    return 4 if a["n"] in PS or SB[a["n"]][1] in (f32, i32) else 2


REF = {"cyc": 1.0, "g": 1.8, "s": 4.3, "pe": 0.5, "lat": 110.0, "rem": 3500.0, "dma": 2200.0, "bw": 180.0, "first": 3000.0}
OTHERS = [{"cyc": 0.83, "pe": 0.42, "g": 1.56, "s": 3.8, "rem": 2500.0, "bw": 200.0, "dma": 1500.0, "lat": 100.0},
          {"cyc": 1.2, "pe": 0.6, "g": 1.9, "s": 5.0, "rem": 3500.0, "bw": 150.0, "lat": 110.0},
          {"cyc": 1.1, "pe": 0.56, "g": 2.08, "s": 6.0, "rem": 3000.0, "lat": 80.0},
          {"cyc": 0.95, "pe": 0.48, "g": 2.0, "s": 2.0, "rem": 4000.0, "lat": 160.0},
          {"cyc": 0.9, "pe": 0.45, "g": 1.4, "s": 4.5, "rem": 5500.0, "lat": 130.0, "first": 5000.0}]


def cost(o, c):
    k, a = o["k"], o["a"]
    if k in ("dma", "send", "arrive"):
        return {"dma": 60.0, "send": 500.0, "arrive": 0.0}[k]
    if k == "mm":
        return max(64, a[2]["w"]) * c["pe"] * (4 if size(a[2]) == 4 else 1) + 10
    w = a[0]["w"]
    if k in ("iota", "sel"):
        return (130 if k == "iota" else 170) + 2 * w * c["cyc"]
    if "win" in a[0]:
        return 50 + c["s"] * w * c["cyc"]
    if k != "set" and "win" in a[1]:
        return 60 + c["g"] * w * c["cyc"]
    if k == "act":
        return 65 + max(64, w) * c["cyc"]
    aps = [x for x in a if isinstance(x, dict) and x["w"] == w]
    f = 0.5 if all(size(x) == 2 for x in aps) else 1.0
    if k == "tt":
        f = 1.0 if any(x["n"] in PS for x in aps[1:]) else 2.0
    return 40 + max(64, w * f) * c["cyc"]


def program(allm):
    L = []

    def op(eng, k, *a):
        L.append({"e": eng, "k": k, "a": a})

    def ts(out, x, s1, o1, s2=None, o2=None): op("V", "ts", out, x, s1, o1, s2, o2)
    def tt(out, x, y, o): op("V", "tt", out, x, y, o)
    def cp(out, x): op("V", "cp", out, x)
    def mset(out, c): op("V", "set", out, c)
    def scan(out, d0, d1, o0, o1): op("V", "scan", out, d0, d1, o0, o1)
    def act(out, x, f, bias=0.0, scale=1.0, acc=None): op("S", "act", out, x, f, bias, scale, acc)
    def mm(out, l, r, st, sp): op("T", "mm", out, l, r, st, sp)
    def grp(out, terms):
        for i, (l, r) in enumerate(terms):
            mm(out, l, r, i == 0, i == len(terms) - 1)
    def iota(out, pat, base, cm): op("G", "iota", out, pat, base, cm)
    def dma(q, out, x, nbytes, after=None): op(q, "dma", out, x, nbytes, after)
    ID = AF.Identity

    dma("Q", v("PT", 2048, M), ("ptr", 2048, M), 128 * 1024)
    dma("S", v("F", M, M + P), ("nw", 0, P), 128 * 512)
    for i in range(4):
        dma("QS"[i % 2], v("PT", 512 * i, 512 * i + 512), ("ptr", 512 * i, 512 * i + 512), 128 * 2048 * (i // 2 + 1))
    dma("Q", v("F", 0, M), ("fr", 0, M), 128 * 4608)
    dma("S", v("F", M + P, E), ("nw", P, 1024), 128 * 1536)
    iota(v("pi", 0, 1), [[0, 1]], 0, 1)
    iota(v("JG"), [[16, 8], [0, 16]], 0, 0)
    iota(v("JR"), [[0, 8], [1, 16]], 0, 0)
    iota(v("J"), [[1, 256]], 0, 0)
    iota(v("CT"), [[0, 16], [1, 16]], 0, 0)
    iota(v("PW"), [[0, 3], [16, 16]], 0, 0)
    iota(v("NA"), [[1, 1024]], M, 0)
    ts(v("ri", 0, 1), v("pi", 0, 1), 15, OP.bitwise_and)
    cp(kc(RF), v("ri", 0, 1))
    cp(kc(PF), v("pi", 0, 1))
    tt(kc(GB), kc(PF), kc(RF), OP.subtract)
    ts(kc(M0), kc(RF), 0.0, OP.is_equal)
    ts(kc(M1E), kc(RF), 1.0, OP.is_equal, float(E), OP.mult)
    ts(kc(OFW), kc(RF), 15.0, OP.is_lt, FRZ, OP.mult)
    act(kc(RP1), kc(RF), ID, bias=1.0)
    act(kc(G15), kc(GB), ID, bias=15.0)
    act(kc(N0M), kc(M0), ID, bias=1.0, scale=-1.0)
    act(kc(OF7), kc(OFW), ID, bias=768.0)
    ts(v("BO"), v("JG"), kc(GB), OP.is_equal)
    act(v("S0f"), v("BO"), ID, scale=kc(M0))
    ts(v("CW"), v("CT"), kc(RF), OP.is_equal, BIG, OP.mult)
    ts(v("CT"), v("CT"), kc(RP1), OP.is_equal, -FRZ, OP.mult)
    tt(v("CW"), v("CW"), v("CT"), OP.add)
    mset(v("A", M, AW), float(E))
    mset(v("F", E, 3336), 99.0)
    ts(v("A", 2048, M), v("PT", 2048, M), kc(M1E), OP.max)
    for lo in (0, 512, 1024, 1536):
        cp(v("A", lo, lo + 512), v("PT", lo, lo + 512))
    dma("Q", v("thi", 0, 1), ("th", 0, 1), 20000, v("A", 0, 8))
    dma("Q", v("hwi", 0, 1), ("hw", 0, 1), 20000, v("A", 0, 8))
    for t in range(NT):
        dma("Q", v("XS", XW * t, XW * t + P), ("nw", P * t, P * t + P), 128 * 512, v("A", 0, 8))
    ts(v("Sel"), v("J", 0, 144), kc(G15), OP.is_equal)
    act(v("Sel2"), v("Sel"), ID, scale=2.0)
    act(v("Seln"), v("Sel"), ID, scale=-1.0)
    ts(v("I"), v("J", 0, 128), kc(PF), OP.is_equal)
    act(v("In"), v("I"), ID, scale=-1.0)
    for i in range(16):
        if i % 3 == 2:
            act(v("xrep", i, 4096, 16), v("F", M, M + P), ID)
        else:
            cp(v("xrep", i, 4096, 16), v("F", M, M + P))
    cp(kc(TH), v("thi", 0, 1))
    cp(kc(HW), v("hwi", 0, 1))
    act(kc(BSG), kc(TH), ID, bias=0.5)
    act(kc(R0S), kc(N0M), ID, scale=16.0)
    act(kc(T1), kc(TH), ID, scale=kc(R0S))
    act(kc(R0B), kc(T1), ID, scale=-1.0, bias=kc(M0))
    for t in range(NT):
        act(kc(FB0 + t), kc(M0), ID, scale=float(E - (M + P * t - P)), bias=0.5 - E)
    act(kc(T2), kc(RF), ID, scale=-1.0, bias=2.0)
    act(kc(BZ1), kc(M0), ID, scale=-200.0, bias=kc(T2))
    act(kc(BZ2), kc(BZ1), ID, bias=-2048.0)
    act(kc(T4), kc(M0), ID, scale=-16.0, bias=kc(T2))
    act(kc(BZ3), kc(T4), ID, bias=-2048.0)
    act(kc(T5), kc(M0), ID, scale=-30720.0 - 2048.0, bias=2048.0)
    act(kc(LB), kc(N0M), ID, scale=float(E))
    for b in range(3):
        act(kc(SL0 + b), kc(RF), ID, bias=16.0 * b + 0.5)
    act(kc(NKB), kc(M0), ID, scale=4000.0)
    act(kc(HSC), kc(M0), ID, scale=30720.0 - 2048.0, bias=2048.0)
    act(kc(T6), kc(M0), ID, scale=30720.0, bias=2048.0)
    act(v("NK", 0, 1024), v("NA"), ID, scale=kc(N0M), bias=kc(NKB))
    mset(v("NK", 1024, 1088), 4000.0)
    iota(v("TA"), [[16, 48], [0, 16]], 0, 0)
    iota(v("TB"), [[0, 48], [1, 16]], 0, 0)
    mset(v("TB", 0, 768, 16), 1.75 * (1 << 20))
    ts(v("PW"), v("PW"), kc(RF), OP.add)
    act(v("DP"), v("PW"), ID, bias=float(DUM + 768))
    act(kc(T3), kc(PF), ID, scale=16.0)
    ts(v("Rn"), v("TA"), kc(T3), OP.is_equal, -1.0, OP.mult)
    mset(v("ONE"), 1.0)
    mset(v("cb", 768, 832), 0.0)
    mset(v("esc", P, SW), 1.0)
    mset(v("Kw", P, XW), -1.0)
    mset(v("Kw", XW + P, 2 * XW), -1.0)
    act(v("CK"), v("NA", 0, 768), ID, scale=0.0)
    cp(v("CK", 0, 768, 16), v("CW", 0, 48))
    for t in range(NT):
        mset(v("XS", XW * t + P, XW * t + SW), 0.0)
        mset(v("XS", XW * t + SW, XW * t + XW), 99.0)
    for name, sc_ in (("BOf", 1.0), ("S0b", kc(M0)), ("BOw", kc(HW)), ("BOk", 1024.0), ("HN", kc(T5)), ("HS", kc(HSC)),
                      ("HS2", kc(T6))):
        act(v(name), v("BO"), ID, scale=sc_)
    act(v("S0n"), v("S0b"), ID, scale=-8192.0)
    act(v("S0h"), v("S0b"), ID, scale=-4096.0)
    act(v("S0k"), v("S0b"), ID, scale=-2048.0)
    ts(v("m1"), v("JR"), kc(RF), OP.is_gt, kc(N0M), OP.mult)
    tt(v("m1"), v("m1"), v("BO"), OP.mult)
    act(v("m2"), v("I"), ID, scale=kc(N0M))
    act(v("m3"), v("m2"), ID, scale=-16.0)
    tt(v("m3"), v("m3"), v("m1"), OP.add)
    act(v("TriF"), v("m3"), ID, scale=4096.0)
    ts(v("m4"), v("JR"), 0.0, OP.is_equal, kc(N0M), OP.mult)
    tt(v("m4"), v("m4"), v("BO"), OP.mult)
    tt(v("m4"), v("m4"), v("m1"), OP.add)
    tt(v("m4"), v("m4"), v("m2"), OP.subtract)
    act(v("ZTh"), v("m4"), ID, scale=0.5)
    act(v("m5"), v("JR"), ID, scale=0.5, bias=7.0)
    tt(v("m5"), v("m5"), v("S0b"), OP.mult)
    tt(v("m6"), v("m5"), v("m2"), OP.add)
    act(v("Ir"), v("m6"), ID, scale=8192.0)
    ts(v("m6"), v("S0b"), 0.5, OP.mult)
    tt(v("m6"), v("m6"), v("m5"), OP.add)
    act(v("CW1"), v("m6"), ID, scale=8192.0)

    def sel(n, i): return v(n, 15 - i, 143 - i)
    def blk(n, h, w=P): return v(n, w * h, w * h + P)
    def bank(n, b): return v(n, 512 * b, 512 * b + P)
    def ow(h): return v("ow", 16 * h, 16 * h + 16)
    AG, FG = v("A", 0, E + 1), v("F", 0, E + 1)
    fill = [0]

    def by_pe(gbuf, g0, n, x, dout):
        rows = list(range(1, 16))
        while rows:
            now, rows = rows[:512 // n], rows[512 // n:]
            hb = 512 * (fill[0] % 2)
            fill[0] += 1
            for j, i in enumerate(now):
                grp(v("PB", hb + n * j, hb + n * j + n), [(v("In"), x), (v("I"), v(gbuf, g0 + i, g0 + 16 * n, 16))])
            act(v("ab", hb, hb + n * len(now)), v("PB", hb, hb + n * len(now)), AF.Abs)
            for j, i in enumerate(now):
                mm(dout, sel("Sel", i), v("ab", hb + n * j, hb + n * j + n), i == 1, i == 15)

    def wrap(h, src):
        scan(blk("scn", h), v("CW"), src, OP.add, OP.min)
        ts(v("kw", 16 * h, 16 * h + 16), v("scn", P * h + 15, P * h + P, 16), kc(OFW), OP.add)

    link = bank("PB", 3)
    grp(link, [(v("S0f"), v("A", 2048, M))])
    nd = [0, 0]
    nh = 3
    for t in range(NT):
        n0 = M + P * t
        modes = allm[t]
        X = v("XS", XW * t, XW * t + XW)
        x = v("XS", XW * t, XW * t + P)
        prev = v("A", n0 - P, n0)
        wrap(0, link)
        if t > 0:
            act(prev, link, ID, scale=kc(M0), bias=kc(LB))
        for h in range(3):
            act(blk("cb", h), ind(AG, v("kw", 16 * h, 16 * h + 16)), ID)
            cp(blk("cu", h), blk("cb", h))
            if h < 2:
                kb = bank("PB", 2)
                grp(kb, [(v("S0f"), blk("cb", h))])
                wrap(h + 1, kb)
        act(blk("fs", 0), prev, AF.Sign, bias=kc(FB0 + t))
        dma("Q", v("A", n0 - P, n0, 1, (1, 128, 16)), v("NK", P * t, P * t + P, 1, (1, 128, 16)), 30000)
        act(v("fs", P, 1024), v("cb", 0, 768), AF.Sign, bias=kc(FB0 + t))
        ts(v("ki"), v("scn", 15, 768, 16), kc(OF7), OP.add)
        ts(v("lo"), v("ki"), 0x10FF, OP.bitwise_and)
        ts(v("ow"), v("lo"), 304.0, OP.min)
        tt(v("s1"), v("lo"), v("PW"), OP.not_equal)
        tt(v("s2"), v("s1"), v("DP"), OP.mult)
        tt(v("s3"), v("s2"), v("ki"), OP.max)
        ts(v("sc"), v("s3"), -768.0, OP.add)
        for h in range(3):
            tt(blk("cval", h), ind(v("NK", P * t, P * t + XW), ow(h)), blk("cb", h), OP.min)
        if t > 0:
            rq = v("req", 48 * t - 48, 48 * t)
            op("X", "arrive", rq, "q%d" % (t - 1))
            qp = v("PM", 0, 48)
            tp, rt = v("PM", 512, 640, 1, (0, 48)), v("rt", 0, 128, 1, (0, 48))
            grp(tp, [(rq, v("I"))])
            act(rt, tp, ID)
            grp(qp, [(v("BOw"), rq)])
            scan(v("qs"), v("CW", 0, 48), qp, OP.add, OP.min)
            ts(v("qi", 0, 3), v("qs", 15, 48, 16), kc(OFW), OP.add)
            ts(v("qj", 0, 3), v("qi", 0, 3), 2047, OP.bitwise_and)
            cp(v("qw", 0, 3), v("qj", 0, 3))
            cp(v("cq"), ind(v("A", 0, 2048), v("qw", 0, 3)))
            for lo, hi in ((0, 512), (512, 768)):
                act(v("dq", lo, hi), ind(FG, v("cq", lo // 16, hi // 16)), ID)
                grp(v("PM", lo, hi), [(rt, v("Rn", lo, hi, 1, (0, 48))), (v("I"), v("dq", lo, hi))])
                act(v("aq", lo, hi), v("PM", lo, hi), AF.Abs)
                grp(v("PM", lo, hi), [(v("S0b"), v("TA", lo, hi)), (v("S0b"), v("TB", lo, hi)), (v("BOk"), v("aq", lo, hi))])
                scan(v("ks", lo, hi), v("CK", lo, hi), v("PM", lo, hi), OP.add, OP.min)
            ts(v("bi", 0, 3), v("ks", 255, 768, 256), kc(OFW), OP.add)
            ts(v("bj", 0, 3), v("bi", 0, 3), 1023, OP.bitwise_and)
            cp(v("bw", 0, 3), v("bj", 0, 3))
            ro = v("out", 48 * t - 48, 48 * t)
            cp(ro, ind(v("dq"), v("bw", 0, 3)))
            op("G", "send", v("rep", 48 * t - 48, 48 * t), ro, "a%d" % (t - 1), -(1 + (t - 1) % (N - 1)))
            pl = v("pl", 0, 3)
            ts(v("xo"), ind(X, pl), 383.5, OP.add)
            for h in range(nh):
                cp(v("cua", 48 * h, 48 * h + 48), ind(v("cb", P * h, P * h + SW), pl))
                act(v("Ga", 768 * h, 768 * h + 768), ind(FG, v("cua", 48 * h, 48 * h + 48)), ID)
        if t + 1 < NT:
            for i in range(16):
                o = 4096 * (t + 1)
                op("G", "sel", v("xrep", o + i, o + 4096, 16), v("F", n0 + P, n0 + 2 * P))
        dh = [v("PD", 0, P), v("PD", 512, 512 + P), v("PD", P, 2 * P)]
        late = []
        for h in range(3):
            for c in range(P // CH):
                s0, mode = CH * c, modes[h * (P // CH) + c]
                dout = v("PD", dh[h]["lo"] + s0, dh[h]["lo"] + s0 + CH)
                if mode in "BL":
                    buf, o = ("Gs", 1024 * (nd[1] % 2)) if mode == "B" else ("G", 16 * s0)
                    for u in (0, 32):
                        act(v(buf, o + 16 * u, o + 16 * u + 512), ind(FG, v("cu", P * h + s0 + u, P * h + s0 + u + 32)), ID)
                    if mode == "B":
                        nd[1] += 1
                        by_pe("Gs", o, CH, v("F", n0 + s0, n0 + s0 + CH), dout)
                    else:
                        late.append((s0, dout))
                    continue
                o = 1024 * (nd[0] % 4)
                nd[0] += 1
                d, ad = v("d", o, o + 16 * CH), v("ad", o, o + 16 * CH)
                for u in (0, 32):
                    tt(v("d", o + 16 * u, o + 16 * u + 512), ind(FG, v("cu", P * h + s0 + u, P * h + s0 + u + 32)),
                       v("xrep", 4096 * t + 16 * (s0 + u), 4096 * t + 16 * (s0 + u) + 512), OP.subtract)
                if mode == "A":
                    act(ad, d, AF.Abs)
                    grp(dout, [(sel("Sel", i), v("ad", o + i, o + 16 * CH, 16)) for i in range(1, 16)])
                else:
                    ts(ad, d, 0.0, OP.max)
                    grp(dout, [(sel("Seln", i), v("d", o + i, o + 16 * CH, 16)) for i in range(1, 16)]
                        + [(sel("Sel2", i), v("ad", o + i, o + 16 * CH, 16)) for i in range(1, 16)])
            if not late:
                act(blk("sg", h, SW), dh[h], AF.Sign, bias=kc(BSG), scale=-1.0)
        if t > 0:
            rp = v("rep", 48 * t - 48, 48 * t)
            op("X", "arrive", rp, "a%d" % (t - 1))
            tt(v("xs"), v("xo"), rp, OP.add)
            for h in range(nh):
                ts(v("xn", 48 * h, 48 * h + 48), v("xs"), 0.5, OP.mult, -192.0, OP.add)
            cp(ind(X, pl), v("xn", 0, 48))
            da = v("PB", 1536, 1536 + 48 * nh)
            by_pe("Ga", 0, 48 * nh, v("xn"), da)
            act(v("sga"), da, AF.Sign, bias=kc(BSG), scale=-1.0)
            for h in range(2):
                cp(ind(v("sg", SW * h, SW * h + SW), pl), v("sga", 48 * h, 48 * h + 48))
        dma("Q", ("yx", P * t, P * t + P), x, 128 * 512)
        cp(v("xc"), x)
        for h in range(3):
            tt(blk("d0", h), ind(X, ow(h)), v("xc"), OP.subtract)
            act(blk("a0", h), blk("d0", h), AF.Abs)
            grp(bank("PM", h % 2), [(v("BO"), blk("a0", h))])
            act(blk("r0", h), bank("PM", h % 2), AF.Relu, bias=kc(R0B), scale=kc(R0S))
        for s0, dout in late:
            by_pe("G", 16 * s0, CH, v("XS", XW * t + s0, XW * t + s0 + CH), dout)
        if late:
            act(blk("sg", 2, SW), dh[2], AF.Sign, bias=kc(BSG), scale=-1.0)
        if t > 0:
            cp(ind(v("sg", SW * 2, SW * 3), pl), v("sga", 96, 144))
        if t + 1 < NT:
            cp(v("F", n0, n0 + P), x)
        U = [bank("PM", 0), bank("PD", 1), bank("PM", 1)]
        H = [bank("PM", 1), bank("PM", 0), bank("PD", 1)]
        Z = [bank("PB", 2), bank("PB", 2), bank("PM", 0)]
        W = [bank("PB", 3), bank("PB", 3), bank("PB", 2)]
        es = [[], [0], [1, 2]]
        for h in range(3):
            col = [(v("TriF"), blk("fs", h + 1)), (v("S0h"), blk("fs", h))]
            wr = [(v("S0n"), blk("e", j)) for j in es[h]]
            grp(U[h], col + [(v("Ir"), blk("r0", h))] + wr)
            act(blk("okn", h), U[h], AF.Sign, bias=-0.5, scale=-1.0)
            old = [(v("S0k"), blk("gs", h - 1))] if h else []
            grp(H[h], old + [(v("HS2" if h else "HS"), blk("sg", h, SW)), (v("HN"), blk("okn", h))])
            if h < 2:
                kwin = v("Kw", XW * h, XW * h + XW)
                tt(blk("Kw", h, XW), H[h], prev if h == 0 else blk("cb", 0), OP.add)
                if h == 0:
                    tt(blk("e", 0), ind(kwin, ow(1)), blk("cb", 0), OP.is_equal)
                tt(blk("e", 1 + h), ind(kwin, ow(2)), blk("cb", 1), OP.is_equal)
            elif t + 1 < NT:
                act(v("esc", 0, P), H[2], AF.Relu, bias=1.0, scale=-1.0)
                scan(v("cnt"), v("ONE"), v("esc"), OP.mult, OP.add)
                for b in range(3):
                    act(v("jk", SW * b, SW * b + SW), v("cnt"), AF.Sign, bias=kc(SL0 + b), scale=-1.0, acc=v("acc", b, b + 1))
                ts(v("pl", 0, 3), v("acc", 0, 3), 0.5, OP.mult, SW / 2.0, OP.add)
                ms = v("msg", 48 * t, 48 * t + 48)
                cp(ms, ind(X, v("pl", 0, 3)))
                op("G", "send", v("req", 48 * t, 48 * t + 48), ms, "q%d" % t, 1 + t % (N - 1))
            act(blk("gs", h), H[h], AF.Sign, bias=0.5, scale=-1.0)
            grp(Z[h], old + [(v("ZTh"), blk("sg", h, SW)), (v("ZTh"), blk("okn", h))])
            act(Z[h], Z[h], AF.Relu, bias=kc(BZ1 + h), scale=-1.0)
            tt(blk("y", h), Z[h], blk("cval", h), OP.mult)
            grp(W[h], col + [(v("CW1"), blk("r0", h))] + wr + [(v("S0h"), blk("gs", h))])
            tt(blk("dlt", h), W[h], blk("cb", h), OP.min)
            tt(ind(v("A"), v("sc", 16 * h, 16 * h + 16)), blk("dlt", h), blk("cval", h), OP.max)
        grp(link, [(v("BOf"), blk("y", h)) for h in range(3)])
    act(v("A", E - P, E), link, ID, scale=kc(M0), bias=kc(LB))
    for q, lo, hi in (("Q", 0, 1536), ("S", 1536, 3072), ("Q", 3072, E)):
        dma(q, ("yp", lo, hi), v("A", lo, hi), 128 * 4 * (hi - lo))
    return L


def touches(o):
    res = []

    def add(a, w):
        if not isinstance(a, dict):
            return
        if "win" in a:
            add(a["win"], w)
            add(a["off"], False)
        elif a["n"] in PS:
            res.append((a["n"], a["lo"] // 512 * 512, (a["hi"] + 511) // 512 * 512, True, 1, True))
        else:
            res.append((a["n"], a["lo"], a["hi"], w, a["st"], a["p"] is None))
    a = o["a"]
    if o["k"] != "send":
        add(a[0], True)
    for i, x in enumerate(a[1:]):
        add(x, o["k"] == "act" and i == 4)
    return res


def clash(x, y):
    if x[1] >= y[2] or y[1] >= x[2] or not (x[3] or y[3]):
        return False
    return not (x[4] == y[4] and x[4] > 1 and (x[1] - y[1]) % x[4] != 0)


def depend(L):
    seen, sent = {}, {}
    for i, o in enumerate(L):
        deps = set()
        tch = touches(o)
        for x in tch:
            for y, j in seen.get(x[0], []):
                if clash(x, y):
                    deps.add(j)
        for x in tch:
            old = seen.get(x[0], [])
            if x[3] and x[4] == 1 and x[5]:
                old = [(y, j) for y, j in old if not (x[1] <= y[1] and y[2] <= x[2])]
            seen[x[0]] = old + [(x, i)]
        deps.discard(i)
        if o["k"] == "send":
            sent[o["a"][2]] = i
        o["deps"] = sorted(deps)
        o["peer"] = sent[o["a"][1]] if o["k"] == "arrive" else None
        a = o["a"][0]
        o["keys"] = (o["e"] + a["n"], (o["e"], a["n"], a.get("lo"))) if isinstance(a, dict) else ("", "")
    return L


def tables(L, c):
    dur = [cost(o, c) for o in L]
    late = [c["dma"] + o["a"][2] / c["bw"] if o["k"] == "dma" else 0.0 for o in L]
    pre, suc = [], [[] for _ in L]
    for i, o in enumerate(L):
        pre.append([(j, 0.0 if o["e"] == "T" and L[j]["e"] == "T" else c["lat"] + late[j]) for j in o["deps"]])
        if o["peer"] is not None:
            pre[i].append((o["peer"], c["rem"] + (c["first"] if o["a"][1] == "q0" else 0.0)))
        for j, w in pre[i]:
            suc[j].append((i, w))
    return dur, late, pre, suc


def replay(L, tab, order):
    dur, late, pre = tab[:3]
    fin, free = [0.0] * len(L), {}
    for i in order:
        st = max([free.get(L[i]["e"], 0.0)] + [fin[j] + w for j, w in pre[i]])
        fin[i] = free[L[i]["e"]] = st + dur[i]
    return max(fin[i] + late[i] for i in range(len(L)))


def schedule(L, tab, bias):
    n = len(L)
    dur, late, pre, suc = tab

    def place(seq, before, head):
        busy, fin = {}, [0.0] * n
        for i in seq:
            st = max([head[i]] + [fin[j] + w for j, w in before[i]])
            slots = busy.setdefault(L[i]["e"], [])
            at = len(slots)
            while at > 0 and slots[at - 1][1] > st:
                at -= 1
            while at < len(slots) and slots[at][0] < st + dur[i]:
                st = max(st, slots[at][1])
                at += 1
            slots.insert(at, (st, st + dur[i]))
            fin[i] = st + dur[i]
        return fin
    more = [max(0.0, dur[i] + bias.get(o["keys"][0], 0.0) + bias.get(o["keys"][1], 0.0)) for i, o in enumerate(L)]
    prio = [more[i] + late[i] + 0.001 for i in range(n)]
    for i in range(n - 1, -1, -1):
        for j, w in pre[i]:
            prio[j] = max(prio[j], more[j] + (1000.0 if L[i]["peer"] == j else w) + prio[i] + 0.001)
    res = []
    for r in range(2):
        fin = place(sorted(range(n), key=lambda i: (-prio[i], i)), pre, [0.0] * n)
        res.append(sorted(range(n), key=lambda i: (fin[i] - dur[i], fin[i], i)))
        if r == 0:
            prio = place(sorted(range(n), key=lambda i: (-fin[i], dur[i] - fin[i], -i)), suc, late)
    return res


def plan():
    L = depend(program(MODES))
    ref, tabs = tables(L, REF), [tables(L, dict(REF, **c)) for c in OTHERS]
    keys = sorted({o["keys"][1] for o in L if o["e"] in "VST" and o["keys"][0] and o["keys"][1][1] not in ("xrep", "K")}, key=str)
    unit = [replay(L, tab, schedule(L, ref, BIAS)[1]) for tab in tabs]

    def score(bias):
        res = []
        for order in schedule(L, ref, bias):
            e = [replay(L, tab, order) / u for tab, u in zip(tabs, unit)]
            res.append((max(e) + sum(e) / len(e), order))
        return min(res)
    rs = numpy.random.RandomState(1)
    bias = dict(BIAS)
    best = score(bias)
    for _ in range(TRIES):
        new = dict(bias)
        for _ in range(int(rs.randint(1, 4))):
            new[keys[int(rs.randint(len(keys)))]] = (-500.0, 0.0, 300.0, 800.0, 1500.0, 3000.0)[int(rs.randint(6))]
        got = score(new)
        if got[0] <= best[0]:
            best, bias = got, new
    return L, best[1], best[0]


PLAN = []


def rank_program(g, core, T, topo):
    rank = T.rank_of(core)
    if rank is None:
        return
    if not PLAN:
        PLAN.append(plan())
    L, order = PLAN[0][0], PLAN[0][1]
    Q = {"V": g.vector, "S": g.scalar, "T": g.tensor, "G": g, "Q": g.sync}

    def ap(a):
        if isinstance(a, tuple):
            return T[a[0]][:, a[1]:a[2]] if a[0] not in ("th", "hw") else T[a[0]][:]
        if not isinstance(a, dict):
            return a
        if "win" in a:
            return ap(a["win"]).indirect(ap(a["off"]))
        cols = slice(a["lo"], a["hi"], a["st"]) if a["st"] > 1 else slice(a["lo"], a["hi"])
        return T[a["n"]][slice(*a["p"]) if a["p"] else slice(None), cols]

    def engines(src):
        both = -1
        for other in T.cores:
            if other != src:
                both &= topo.mask(src, other)
        return both
    mark, count, know, clock, total = {}, {}, {e: {} for e in Q}, {}, {}
    nd = [0]
    for i in order:
        o = L[i]
        e, k, a = o["e"], o["k"], o["a"]
        if k == "arrive":
            src = T.cores[(rank - L[o["peer"]]["a"][3]) % N]
            mark[i] = (a[1], bin(engines(src)).count("1"))
            clock[i] = {}
            total[a[1]] = mark[i][1]
            continue
        q, kn = Q[e], know[e]
        for j in sorted(o["deps"], key=lambda j: -mark[j][1]):
            if e == "T" and L[j]["e"] == "T":
                continue
            s, n = mark[j]
            if kn.get(s, 0) < n:
                q.wait_ge(T.sem[s], n)
                kn[s] = n
                for s2, n2 in clock[j].items():
                    kn[s2] = max(kn.get(s2, 0), n2)
        clock[i] = dict(kn)
        x = [ap(z) for z in a]
        if k == "dma":
            s = "d%d" % nd[0]
            nd[0] += 1
            q.dma_start(x[0], x[1]).then_inc(T.sem[s], 16)
            mark[i] = (s, 16)
            total[s] = 16
            continue
        if k == "send":
            dst, m = T.cores[(rank + a[3]) % N], engines(core)
            g.remote_dma(x[0], x[1], T.sem[a[2]], T.sem.lo, topo.addr(dst)[1], topo.addr(dst)[0], m)
            total["lo"] = total.get("lo", 0) + bin(m).count("1")
            mark[i] = ("lo", total["lo"])
            continue
        if k == "ts":
            ins = q.tensor_scalar(x[0], x[1], x[2], None, x[3]) if x[5] is None else q.tensor_scalar(x[0], x[1], x[2], x[4], x[3], x[5])
        elif k == "tt":
            ins = q.tensor_tensor(x[0], x[1], x[2], x[3])
        elif k == "cp":
            ins = q.tensor_copy(x[0], x[1])
        elif k == "set":
            ins = q.memset(x[0], x[1])
        elif k == "scan":
            ins = q.tensor_tensor_scan(x[0], x[1], x[2], 0.0, x[3], x[4])
        elif k == "act":
            ins = q.activation(x[0], x[1], x[2], bias=x[3], scale=x[4], accum_out=x[5])
        elif k == "mm":
            ins = q.matmul(x[0], x[1], x[2], x[3], x[4])
        elif k == "iota":
            if SB[a[0]["n"]][1] == i32:
                ins = g.iota(x[0], x[1], x[2], x[3])
            else:
                ins = g.iota(x[0], x[1], x[2], x[3], allow_small_or_imprecise_dtypes=True)
        else:
            ins = g.affine_select(x[0], x[1], [[0, P]], OP.is_ge, 0.0, 0, 0)
        count[e] = count.get(e, 0) + 1
        ins.then_inc(T.sem[e], 1)
        mark[i] = (e, count[e])
        total[e] = count[e]
    for s, n in total.items():
        g.wait_ge(T.sem[s], n)
